import numpy as np
import ml_dtypes


def mxq(x, axis, fmt="e4m3"):
    dtype, down = {"e4m3": (ml_dtypes.float8_e4m3fn, 7), "e5m2": (ml_dtypes.float8_e5m2, 14)}[fmt]
    v = np.moveaxis(np.asarray(x, np.float32).astype(ml_dtypes.bfloat16).astype(np.float64), axis, -1)
    blocks = v.reshape(v.shape[:-1] + (-1, 32))
    amax = np.abs(blocks).max(-1, keepdims=True)
    byte = np.maximum(np.where(amax > 0, np.frexp(amax)[1] - 1 + 127, 0) - down, 1)
    scale = np.exp2(byte - 127.0)
    codes = (blocks / scale).astype(np.float32).astype(dtype).astype(np.float64)
    return np.moveaxis((codes * scale).reshape(v.shape), -1, axis)


WIDE = False


def mx_kscale(k):
    if not WIDE:
        return np.ones(k)
    levels = np.array([24, -24, 12, -12, 0])
    if k % 512:
        return np.exp2(np.random.permutation(np.resize(levels, k // 32))).repeat(32)
    a = np.empty((k // 512, 16))
    for p in range(k // 512):
        a[p, :8] = np.random.permutation(np.resize(levels, 8))
        for g in range(8):
            far = levels[np.abs(levels - a[p, g]) >= 10]
            a[p, g + 8] = far[np.random.randint(len(far))]
    return np.exp2(a.ravel()).repeat(32)


def f64(x):
    return np.asarray(x).astype(np.float64)


def striped(idx):
    return np.tile(idx.reshape(-1, 16).T, (8, 1)).astype(np.uint16)


def unstriped(offs):
    return offs[:16].T.reshape(-1).astype(np.int64)


E2M1 = np.array([0.0, 0.5, 1.0, 1.5, 2.0, 3.0, 4.0, 6.0, -0.0, -0.5, -1.0, -1.5, -2.0, -3.0, -4.0, -6.0])


def pack_weight(w, fmt):
    k, n = w.shape
    w = f64(np.asarray(w, np.float32).astype(ml_dtypes.bfloat16)).reshape(k // 32, 32, n)
    amax = np.abs(w).max(1)
    if fmt == "e4m3":
        byte = np.frexp(amax)[1] - 1 + 127 - 7
    else:
        mant, ex = np.frexp(amax / 6.0)
        byte = np.where(mant > 0.5, ex, ex - 1) + 127
    byte = np.clip(np.where(amax > 0, byte, 1), 1, 254)
    scaled = (w * np.exp2(127.0 - byte)[:, None, :]).reshape(k, n).astype(np.float32)
    by_word = np.ascontiguousarray(scaled.reshape(k // 512, 128, 4, n).transpose(0, 1, 3, 2))
    if fmt == "e4m3":
        words = by_word.astype(ml_dtypes.float8_e4m3fn).view(np.uint8)
    else:
        c = by_word.astype(ml_dtypes.float4_e2m1fn).view(np.uint8) & 0xF
        words = (c[..., 0::2] | (c[..., 1::2] << 4)).reshape(k // 512, 128, 2 * n)
    return np.ascontiguousarray(words), np.ascontiguousarray(byte.astype(np.uint8).reshape(k // 512, 16, n))


def unpack_weight(words, scales, fmt):
    g, _, n = scales.shape
    words = np.ascontiguousarray(words).reshape(g, 128, n, -1)
    if fmt == "e4m3":
        vals = words.view(ml_dtypes.float8_e4m3fn).astype(np.float64)
    else:
        nib = np.empty((g, 128, n, 4), np.uint8)
        nib[..., 0::2] = words & 0xF
        nib[..., 1::2] = words >> 4
        vals = E2M1[nib]
    vals = vals * np.repeat(np.exp2(scales.astype(np.float64) - 127.0), 8, axis=1)[..., None]
    return vals.transpose(0, 1, 3, 2).reshape(g * 512, n)


def pack_table4(v):
    words, scales = pack_weight(v, "e2m1")
    g, t = words.shape[0] // 2, v.shape[1]
    return np.ascontiguousarray(words.reshape(g, 2, 128, t, 2).transpose(0, 2, 3, 1, 4).reshape(g, 128, t, 4)), scales


def unpack_table4(words, scales):
    g, _, t, _ = words.shape
    return unpack_weight(words.reshape(g, 128, t, 2, 2).transpose(0, 3, 1, 2, 4).reshape(2 * g, 128, 2 * t), scales, "e2m1")


def silu(f):
    return f / (1.0 + np.exp(-np.maximum(f, -700.0)))


K, R, N, T, J = 1024, 1024, 256, 1024, 512


def setup_inputs():
    n = np.random.standard_normal
    s = mx_kscale(K)[:, None]
    u = mx_kscale(R)[:, None]
    p_tab = pack_table4(n((K, T)) * s)
    p_w0 = pack_weight(n((K, R)) / np.sqrt(3 * K) / s, "e2m1")
    p_w1 = pack_weight(n((K, R)) / np.sqrt(3 * K) / s, "e4m3")
    p_wd = pack_weight(n((R, N)) / np.sqrt(R) / u, "e2m1")
    return {
        "tab_words": p_tab[0],
        "tab_scales": p_tab[1],
        "w0_words": p_w0[0],
        "w0_scales": p_w0[1],
        "w1_words": p_w1[0],
        "w1_scales": p_w1[1],
        "w2": (n((K, R)) / np.sqrt(3 * K) / s).astype(np.float32),
        "sm": (np.random.uniform(0.5, 2.0, R) * u[:, 0]).astype(np.float32),
        "wd_words": p_wd[0],
        "wd_scales": p_wd[1],
        "b": (0.3 * n(N)).astype(np.float32),
        "offs": striped(np.concatenate([np.random.permutation(T)[:J] for _ in range(3)])),
    }


def reference(tab_words, tab_scales, w0_words, w0_scales, w1_words, w1_scales, w2, sm, wd_words, wd_scales, b, offs):
    idx = unstriped(offs).reshape(3, J)
    tab_ = unpack_table4(tab_words, tab_scales)[:, idx]
    w0_ = unpack_weight(w0_words, w0_scales, "e2m1")
    w1_ = unpack_weight(w1_words, w1_scales, "e4m3")
    w2_ = mxq(f64(w2), 0, "e4m3")
    a = w0_.T @ tab_[:, 0] + w1_.T @ tab_[:, 1] + w2_.T @ tab_[:, 2]
    h = f64(sm)[:, None] * silu(a)
    h_ = mxq(h, 0, "e4m3")
    wd_ = unpack_weight(wd_words, wd_scales, "e2m1")
    y = wd_.T @ h_
    return y + f64(b)[:, None]

@@ -1,0 +1,259 @@
+from contextlib import ExitStack
+
+import concourse.mybir as mybir
+from concourse.masks import make_identity
+
+K, R, N, T, J = 1024, 1024, 256, 1024, 512
+FLOPS = 2 * J * (3 * K * R + R * N)
+
+F32 = mybir.dt.float32
+BF16 = mybir.dt.bfloat16
+I32 = mybir.dt.int32
+U32 = mybir.dt.uint32
+U16 = mybir.dt.uint16
+U8 = mybir.dt.uint8
+FP8X4 = mybir.dt.float8_e4m3fn_x4
+FP4X4 = mybir.dt.float4_e2m1fn_x4
+ACT = mybir.ActivationFunctionType
+MULT = mybir.AluOpType.mult
+
+P = 128
+HALF = 512
+
+
+def tile_list_rvq_silu_bias_kernel(
+    tc, tab_words, tab_scales, w0_words, w0_scales, w1_words, w1_scales, w2, sm, wd_words, wd_scales, b, offs, out
+):
+    nc = tc.nc
+    with ExitStack() as ctx:
+        keep = ctx.enter_context(tc.tile_pool(name="keep", bufs=1))
+        psum = ctx.enter_context(tc.psum_pool(name="psum", bufs=1))
+
+        offsets = keep.tile([P, 3 * J // 16], U16, name="offsets")
+        tabw = keep.tile([P, T], I32, name="tabw", align_bytes=64)
+        tabs = keep.tile([P, T], U8, name="tabs", align_bytes=64)
+        w0w = keep.tile([P, 2, 2 * R], U8, name="w0w", align_bytes=64)
+        w0s = keep.tile([P, 2, R], U8, name="w0s", align_bytes=64)
+        w1w = keep.tile([P, 2, 4 * R], U8, name="w1w", align_bytes=64)
+        w1s = keep.tile([P, 2, R], U8, name="w1s", align_bytes=64)
+        wdw = keep.tile([P, 2, 2 * N], U8, name="wdw", align_bytes=64)
+        wds = keep.tile([P, 2, N], U8, name="wds", align_bytes=64)
+        smt = keep.tile([P, 2, 4], F32, name="smt")
+        bias = keep.tile([P, 2], F32, name="bias")
+        ident = keep.tile([P, P], F32, name="ident", align_bytes=64)
+        warm = keep.tile([P, 2], F32, name="warm")
+        gw = [keep.tile([P, J], U32, name=f"gw{g}", align_bytes=64) for g in range(3)]
+        vw = [keep.tile([P, 2, 2 * J], U8, name=f"vw{g}", align_bytes=64) for g in range(3)]
+        gs = keep.tile([P, 3 * J], U8, name="gs", align_bytes=64)
+        gs1 = keep.tile([P, 3 * J], U8, name="gs1", align_bytes=64)
+        raw = {}
+        grp = {}
+        w2c = {}
+        w2s = {}
+        for hb in range(2):
+            for a in range(2):
+                raw[hb, a] = keep.tile([P, 4, HALF], F32, name=f"raw{hb}{a}", align_bytes=64)
+                grp[hb, a] = keep.tile([P, HALF, 4], BF16, name=f"grp{hb}{a}", align_bytes=64)
+                w2c[hb, a] = keep.tile([P, HALF], U32, name=f"w2c{hb}{a}", align_bytes=64)
+                w2s[hb, a] = keep.tile([P, HALF], U8, name=f"w2s{hb}{a}", align_bytes=64)
+        hgrp = [keep.tile([P, J, 4], BF16, name=f"hgrp{hb}", align_bytes=64) for hb in range(2)]
+        hc = [keep.tile([P, J], U32, name=f"hc{hb}", align_bytes=64) for hb in range(2)]
+        hs = [keep.tile([P, J], U8, name=f"hs{hb}", align_bytes=64) for hb in range(2)]
+        acc = {}
+        for hb in range(2):
+            for jt in range(4):
+                acc[hb, jt] = psum.tile([P, HALF], F32, name=f"acc{hb}{jt}", tag=f"bank{hb}{jt}")
+
+        def load_planes(plane, scales):
+            for q in range(4):
+                nc.sync.dma_start(
+                    out=plane[32 * q : 32 * q + 4, :, :].bitcast(I32),
+                    in_=scales[:, 4 * q : 4 * q + 4, :].bitcast(I32).rearrange("a r c -> r a c"),
+                )
+
+        def load_w2(hb, a):
+            rows = w2[HALF * a : HALF * (a + 1), HALF * hb : HALF * (hb + 1)]
+            nc.sync.dma_start(out=raw[hb, a][:], in_=rows.rearrange("(p i) c -> p i c", i=4))
+
+        def load_w1(a):
+            nc.sync.dma_start(
+                out=w1w[:, a, :].bitcast(I32), in_=w1_words[a].rearrange("p r i -> p (r i)").bitcast(I32)
+            )
+
+        def gather_scales(g, j0, j1):
+            lst = offsets[:, (g * J + j0) // 16 : (g * J + j1) // 16]
+            nc.vector.tensor_copy(out=gs[:, g * J + j0 : g * J + j1], in_=tabs[:].indirect(lst))
+
+        def gather_words(g, j0, j1):
+            lst = offsets[:, (g * J + j0) // 16 : (g * J + j1) // 16]
+            nc.vector.tensor_copy(out=gw[g][:, j0:j1], in_=tabw[:].bitcast(U32).indirect(lst))
+
+        def part_words(g, j0, j1):
+            nc.vector.tensor_copy(
+                out=vw[g][:, :, 2 * j0 : 2 * j1].bitcast(U16),
+                in_=gw[g][:, j0:j1].bitcast(U16).rearrange("p (j d) -> p d j", d=2),
+            )
+
+        def shift_scales(c0, c1):
+            nc.gpsimd.dma_start(out=gs1[0:112, c0:c1].bitcast(I32), in_=gs[4:116, c0:c1].bitcast(I32))
+
+        def cast_w2(hb, a, on_vector):
+            dst = grp[hb, a][:].rearrange("p (c e) i -> p c i e", e=4)
+            src = raw[hb, a][:].rearrange("p i (c e) -> p c i e", e=4)
+            if on_vector:
+                nc.vector.tensor_copy(out=dst, in_=src)
+            else:
+                nc.scalar.copy(out=dst, in_=src)
+
+        def quantize_w2(hb, a):
+            nc.vector.quantize_mx(
+                out=w2c[hb, a][:].bitcast(FP8X4), scales=w2s[hb, a][:], in_=grp[hb, a][:].rearrange("p c i -> p (c i)")
+            )
+
+        def first_layer(g, a, hb, jt):
+            cols = slice(HALF * hb, HALF * (hb + 1))
+            if g == 0:
+                rhs, rhs_scale = w0w[:, a, 2 * cols.start : 2 * cols.stop].bitcast(FP4X4), w0s[:, a, cols]
+            elif g == 1:
+                rhs, rhs_scale = w1w[:, a, 4 * cols.start : 4 * cols.stop].bitcast(FP8X4), w1s[:, a, cols]
+            else:
+                rhs, rhs_scale = w2c[hb, a][:].bitcast(FP8X4), w2s[hb, a][:]
+            plane = gs if a == 0 else gs1
+            nc.tensor.matmul_mx(
+                out=acc[hb, jt][:],
+                lhsT=vw[g][:, a, 2 * P * jt : 2 * P * (jt + 1)].bitcast(FP4X4),
+                lhsT_scale=plane[:, g * J + P * jt : g * J + P * (jt + 1)],
+                rhs=rhs,
+                rhs_scale=rhs_scale,
+                start=(g == 0 and a == 0),
+                stop=(g == 2 and a == 1),
+            )
+
+        act = {}
+        turned = {}
+
+        def silu(hb, jt):
+            act[hb, jt] = keep.tile([P, 4, P], F32, name=f"act{hb}{jt}", align_bytes=64)
+            nc.scalar.activation(
+                out=act[hb, jt][:], in_=acc[hb, jt][:].rearrange("p (q i) -> p i q", i=4), func=ACT.Silu
+            )
+
+        def turn(hb, jt):
+            turned[hb, jt] = psum.tile([P, 4, P], F32, name=f"turned{hb}{jt}", tag=f"bank{hb}{jt}")
+            for i in range(4):
+                nc.tensor.transpose(turned[hb, jt][:, i, :], act[hb, jt][:, i, :], ident[:])
+
+        def smooth(hb, jt):
+            nc.vector.tensor_tensor(
+                out=hgrp[hb][:, P * jt : P * (jt + 1), :],
+                in0=turned[hb, jt][:].rearrange("p i j -> p j i"),
+                in1=smt[:, hb, :].unsqueeze(1).to_broadcast([P, P, 4]),
+                op=MULT,
+            )
+
+        def quantize_h(hb, jt):
+            cols = slice(P * jt, P * (jt + 1))
+            nc.vector.quantize_mx(
+                out=hc[hb][:, cols].bitcast(FP8X4),
+                scales=hs[hb][:, cols],
+                in_=hgrp[hb][:, cols, :].rearrange("p j i -> p (j i)"),
+            )
+
+        def second_layer(jt):
+            cols = slice(P * jt, P * (jt + 1))
+            y = psum.tile([P, 2, P], F32, name=f"y{jt}", tag=f"bank0{jt}")
+            res = keep.tile([P, 2, P], F32, name=f"res{jt}")
+            for nt in range(2):
+                for hb in range(2):
+                    nc.tensor.matmul_mx(
+                        out=y[:, nt, :],
+                        lhsT=wdw[:, hb, 2 * P * nt : 2 * P * (nt + 1)].bitcast(FP4X4),
+                        lhsT_scale=wds[:, hb, P * nt : P * (nt + 1)],
+                        rhs=hc[hb][:, cols].bitcast(FP8X4),
+                        rhs_scale=hs[hb][:, cols],
+                        start=(hb == 0),
+                        stop=(hb == 1),
+                    )
+            for nt in range(2):
+                nc.scalar.activation(
+                    out=res[:, nt, :], in_=y[:, nt, :], func=ACT.Identity, bias=bias[:, nt : nt + 1]
+                )
+            nc.sync.dma_start(out=out.rearrange("(nt p) j -> p nt j", p=P)[:, :, cols], in_=res[:])
+
+        nc.vector.memset(tabs[:].bitcast(I32), 0)
+        nc.vector.memset(w0s[:].rearrange("p a c -> p (a c)").bitcast(I32), 0)
+        nc.vector.memset(warm[:], 0.0)
+        nc.vector.memset(gs1[:].bitcast(I32), 0)
+        nc.vector.memset(w1s[:].rearrange("p a c -> p (a c)").bitcast(I32), 0)
+        nc.vector.memset(wds[:].rearrange("p a c -> p (a c)").bitcast(I32), 0)
+        nc.scalar.activation(out=warm[:, 1:2], in_=warm[:, 0:1], func=ACT.Silu)
+        make_identity(nc, ident[:])
+
+        nc.sync.dma_start(offsets[:], offs)
+        for q in range(4):
+            nc.sync.dma_start(
+                out=tabs[32 * q : 32 * q + 8, :].bitcast(I32), in_=tab_scales[:, 4 * q : 4 * q + 4, :].bitcast(I32)
+            )
+        nc.sync.dma_start(out=tabw[:], in_=tab_words[0].rearrange("p t f -> p (t f)").bitcast(I32))
+        load_planes(w0s, w0_scales)
+        for a in range(2):
+            nc.sync.dma_start(out=w0w[:, a, :].bitcast(I32), in_=w0_words[a].bitcast(I32))
+
+        gather_scales(0, 0, J)
+        shift_scales(0, J)
+        load_w2(0, 0)
+        load_planes(w1s, w1_scales)
+        load_w1(0)
+        nc.sync.dma_start(out=smt[:], in_=sm.rearrange("(h p i) -> p h i", h=2, i=4))
+        gather_words(0, 0, J // 2)
+        part_words(0, 0, J // 2)
+        gather_words(0, J // 2, J)
+        part_words(0, J // 2, J)
+        gather_scales(1, 0, J)
+        gather_scales(2, 0, J)
+        shift_scales(J, 3 * J)
+        load_w2(0, 1)
+        load_w1(1)
+        load_w2(1, 0)
+        load_w2(1, 1)
+        load_planes(wds, wd_scales)
+        nc.sync.dma_start(out=wdw[:].bitcast(I32), in_=wd_words.bitcast(I32).rearrange("a p c -> p a c"))
+        with nc.allow_non_contiguous_dma(reason="one bias value to a partition"):
+            nc.sync.dma_start(out=bias[:], in_=b.rearrange("(nt p) -> p nt", p=P))
+        gather_words(1, 0, J)
+        cast_w2(0, 0, False)
+        gather_words(2, 0, J)
+        part_words(1, 0, J)
+        quantize_w2(0, 0)
+        part_words(2, 0, J)
+        cast_w2(0, 1, False)
+        quantize_w2(0, 1)
+
+        for g in range(2):
+            for a in range(2):
+                for jt in range(4):
+                    for hb in range(2):
+                        first_layer(g, a, hb, jt)
+        for a in range(2):
+            for jt in range(4):
+                first_layer(2, a, 0, jt)
+        cast_w2(1, 0, False)
+        quantize_w2(1, 0)
+        for jt in range(4):
+            silu(0, jt)
+        cast_w2(1, 1, True)
+        for jt in range(4):
+            first_layer(2, 0, 1, jt)
+        quantize_w2(1, 1)
+        for jt in range(4):
+            turn(0, jt)
+            smooth(0, jt)
+        for jt in range(4):
+            first_layer(2, 1, 1, jt)
+            quantize_h(0, jt)
+        for jt in range(4):
+            silu(1, jt)
+            turn(1, jt)
+            smooth(1, jt)
+            quantize_h(1, jt)
+            second_layer(jt)

@@ -19,6 +19,7 @@ MULT = mybir.AluOpType.mult
 
 P = 128
 HALF = 512
+JH = J // 2
 
 
 def tile_list_rvq_silu_bias_kernel(
@@ -31,21 +32,20 @@ def tile_list_rvq_silu_bias_kernel(
 
         offsets = keep.tile([P, 3 * J // 16], U16, name="offsets")
         tabw = keep.tile([P, T], I32, name="tabw", align_bytes=64)
-        tabs = keep.tile([P, T], U8, name="tabs", align_bytes=64)
+        tabs = keep.tile([P, 2, T], U8, name="tabs", align_bytes=64)
+        wdw = keep.tile([P, 2, 2 * N], U8, name="wdw", align_bytes=64)
+        wds = keep.tile([P, 2, N], U8, name="wds", align_bytes=64)
         w0w = keep.tile([P, 2, 2 * R], U8, name="w0w", align_bytes=64)
         w0s = keep.tile([P, 2, R], U8, name="w0s", align_bytes=64)
         w1w = keep.tile([P, 2, 4 * R], U8, name="w1w", align_bytes=64)
         w1s = keep.tile([P, 2, R], U8, name="w1s", align_bytes=64)
-        wdw = keep.tile([P, 2, 2 * N], U8, name="wdw", align_bytes=64)
-        wds = keep.tile([P, 2, N], U8, name="wds", align_bytes=64)
         smt = keep.tile([P, 2, 4], F32, name="smt")
         bias = keep.tile([P, 2], F32, name="bias")
         ident = keep.tile([P, P], F32, name="ident", align_bytes=64)
         warm = keep.tile([P, 2], F32, name="warm")
-        gw = [keep.tile([P, J], U32, name=f"gw{g}", align_bytes=64) for g in range(3)]
+        gw = {}
         vw = [keep.tile([P, 2, 2 * J], U8, name=f"vw{g}", align_bytes=64) for g in range(3)]
-        gs = keep.tile([P, 3 * J], U8, name="gs", align_bytes=64)
-        gs1 = keep.tile([P, 3 * J], U8, name="gs1", align_bytes=64)
+        gs = {}
         raw = {}
         grp = {}
         w2c = {}
@@ -53,7 +53,7 @@ def tile_list_rvq_silu_bias_kernel(
         for hb in range(2):
             for a in range(2):
                 raw[hb, a] = keep.tile([P, 4, HALF], F32, name=f"raw{hb}{a}", align_bytes=64)
-                grp[hb, a] = keep.tile([P, HALF, 4], BF16, name=f"grp{hb}{a}", align_bytes=64)
+                grp[hb, a] = keep.tile([P, HALF, 4], BF16, name=f"grp{hb}{a}", tag=f"grp{hb}{a}", align_bytes=64)
                 w2c[hb, a] = keep.tile([P, HALF], U32, name=f"w2c{hb}{a}", align_bytes=64)
                 w2s[hb, a] = keep.tile([P, HALF], U8, name=f"w2s{hb}{a}", align_bytes=64)
         hgrp = [keep.tile([P, J, 4], BF16, name=f"hgrp{hb}", align_bytes=64) for hb in range(2)]
@@ -75,31 +75,28 @@ def tile_list_rvq_silu_bias_kernel(
             rows = w2[HALF * a : HALF * (a + 1), HALF * hb : HALF * (hb + 1)]
             nc.sync.dma_start(out=raw[hb, a][:], in_=rows.rearrange("(p i) c -> p i c", i=4))
 
-        def load_w1(a):
-            nc.sync.dma_start(
-                out=w1w[:, a, :].bitcast(I32), in_=w1_words[a].rearrange("p r i -> p (r i)").bitcast(I32)
-            )
+        def places(g, j0, j1):
+            return offsets[:, (g * J + j0) // 16 : (g * J + j1) // 16]
 
-        def gather_scales(g, j0, j1):
-            lst = offsets[:, (g * J + j0) // 16 : (g * J + j1) // 16]
-            nc.vector.tensor_copy(out=gs[:, g * J + j0 : g * J + j1], in_=tabs[:].indirect(lst))
+        def gather_scales(g, a, j0, j1, dst):
+            for jt in range(j0 // P, j1 // P):
+                gs[g, a, jt] = dst[:, P * jt - j0 : P * (jt + 1) - j0]
+            nc.vector.tensor_copy(out=dst, in_=tabs[:, a, :].indirect(places(g, j0, j1)))
 
-        def gather_words(g, j0, j1):
-            lst = offsets[:, (g * J + j0) // 16 : (g * J + j1) // 16]
-            nc.vector.tensor_copy(out=gw[g][:, j0:j1], in_=tabw[:].bitcast(U32).indirect(lst))
+        def gather_words(g, h, dst):
+            gw[g, h] = dst
+            lst = places(g, JH * h, JH * (h + 1))
+            nc.vector.tensor_copy(out=dst.bitcast(U32), in_=tabw[:].bitcast(U32).indirect(lst))
 
-        def part_words(g, j0, j1):
+        def part_words(g, h):
             nc.vector.tensor_copy(
-                out=vw[g][:, :, 2 * j0 : 2 * j1].bitcast(U16),
-                in_=gw[g][:, j0:j1].bitcast(U16).rearrange("p (j d) -> p d j", d=2),
+                out=vw[g][:, :, 2 * JH * h : 2 * JH * (h + 1)].bitcast(U16),
+                in_=gw[g, h].bitcast(U16).rearrange("p (j d) -> p d j", d=2),
             )
 
-        def shift_scales(c0, c1):
-            nc.gpsimd.dma_start(out=gs1[0:112, c0:c1].bitcast(I32), in_=gs[4:116, c0:c1].bitcast(I32))
-
-        def cast_w2(hb, a, on_vector):
-            dst = grp[hb, a][:].rearrange("p (c e) i -> p c i e", e=4)
-            src = raw[hb, a][:].rearrange("p i (c e) -> p c i e", e=4)
+        def cast_w2(hb, a, c0, c1, on_vector):
+            dst = grp[hb, a][:, c0:c1, :].rearrange("p (c e) i -> p c i e", e=4)
+            src = raw[hb, a][:, :, c0:c1].rearrange("p i (c e) -> p c i e", e=4)
             if on_vector:
                 nc.vector.tensor_copy(out=dst, in_=src)
             else:
@@ -118,11 +115,10 @@ def tile_list_rvq_silu_bias_kernel(
                 rhs, rhs_scale = w1w[:, a, 4 * cols.start : 4 * cols.stop].bitcast(FP8X4), w1s[:, a, cols]
             else:
                 rhs, rhs_scale = w2c[hb, a][:].bitcast(FP8X4), w2s[hb, a][:]
-            plane = gs if a == 0 else gs1
             nc.tensor.matmul_mx(
                 out=acc[hb, jt][:],
                 lhsT=vw[g][:, a, 2 * P * jt : 2 * P * (jt + 1)].bitcast(FP4X4),
-                lhsT_scale=plane[:, g * J + P * jt : g * J + P * (jt + 1)],
+                lhsT_scale=gs[g, a, jt],
                 rhs=rhs,
                 rhs_scale=rhs_scale,
                 start=(g == 0 and a == 0),
@@ -151,8 +147,8 @@ def tile_list_rvq_silu_bias_kernel(
                 op=MULT,
             )
 
-        def quantize_h(hb, jt):
-            cols = slice(P * jt, P * (jt + 1))
+        def quantize_h(hb, jt0, jt1):
+            cols = slice(P * jt0, P * jt1)
             nc.vector.quantize_mx(
                 out=hc[hb][:, cols].bitcast(FP8X4),
                 scales=hs[hb][:, cols],
@@ -180,80 +176,93 @@ def tile_list_rvq_silu_bias_kernel(
                 )
             nc.sync.dma_start(out=out.rearrange("(nt p) j -> p nt j", p=P)[:, :, cols], in_=res[:])
 
-        nc.vector.memset(tabs[:].bitcast(I32), 0)
-        nc.vector.memset(w0s[:].rearrange("p a c -> p (a c)").bitcast(I32), 0)
+        nc.vector.memset(tabs[:, 0, :].bitcast(I32), 0)
+        nc.gpsimd.memset(tabs[:, 1, :].bitcast(I32), 0)
         nc.vector.memset(warm[:], 0.0)
-        nc.vector.memset(gs1[:].bitcast(I32), 0)
+        nc.vector.memset(w0s[:].rearrange("p a c -> p (a c)").bitcast(I32), 0)
         nc.vector.memset(w1s[:].rearrange("p a c -> p (a c)").bitcast(I32), 0)
         nc.vector.memset(wds[:].rearrange("p a c -> p (a c)").bitcast(I32), 0)
         nc.scalar.activation(out=warm[:, 1:2], in_=warm[:, 0:1], func=ACT.Silu)
         make_identity(nc, ident[:])
 
         nc.sync.dma_start(offsets[:], offs)
-        for q in range(4):
-            nc.sync.dma_start(
-                out=tabs[32 * q : 32 * q + 8, :].bitcast(I32), in_=tab_scales[:, 4 * q : 4 * q + 4, :].bitcast(I32)
-            )
+        load_planes(tabs, tab_scales)
         nc.sync.dma_start(out=tabw[:], in_=tab_words[0].rearrange("p t f -> p (t f)").bitcast(I32))
+        nc.sync.dma_start(out=w0w[:, 0, :].bitcast(I32), in_=w0_words[0].bitcast(I32))
         load_planes(w0s, w0_scales)
-        for a in range(2):
-            nc.sync.dma_start(out=w0w[:, a, :].bitcast(I32), in_=w0_words[a].bitcast(I32))
-
-        gather_scales(0, 0, J)
-        shift_scales(0, J)
+        nc.sync.dma_start(out=w0w[:, 1, :].bitcast(I32), in_=w0_words[1].bitcast(I32))
         load_w2(0, 0)
         load_planes(w1s, w1_scales)
-        load_w1(0)
-        nc.sync.dma_start(out=smt[:], in_=sm.rearrange("(h p i) -> p h i", h=2, i=4))
-        gather_words(0, 0, J // 2)
-        part_words(0, 0, J // 2)
-        gather_words(0, J // 2, J)
-        part_words(0, J // 2, J)
-        gather_scales(1, 0, J)
-        gather_scales(2, 0, J)
-        shift_scales(J, 3 * J)
+        nc.sync.dma_start(out=w1w[:].bitcast(I32), in_=w1_words.rearrange("a p r i -> p a (r i)").bitcast(I32))
         load_w2(0, 1)
-        load_w1(1)
         load_w2(1, 0)
+        nc.sync.dma_start(out=smt[:], in_=sm.rearrange("(h p i) -> p h i", h=2, i=4))
         load_w2(1, 1)
         load_planes(wds, wd_scales)
         nc.sync.dma_start(out=wdw[:].bitcast(I32), in_=wd_words.bitcast(I32).rearrange("a p c -> p a c"))
         with nc.allow_non_contiguous_dma(reason="one bias value to a partition"):
             nc.sync.dma_start(out=bias[:], in_=b.rearrange("(nt p) -> p nt", p=P))
-        gather_words(1, 0, J)
-        cast_w2(0, 0, False)
-        gather_words(2, 0, J)
-        part_words(1, 0, J)
-        quantize_w2(0, 0)
-        part_words(2, 0, J)
-        cast_w2(0, 1, False)
-        quantize_w2(0, 1)
 
-        for g in range(2):
+        first_scales = keep.tile([P, J], U8, name="first_scales", align_bytes=64)
+        first_words = [keep.tile([P, 4 * JH], U8, name=f"first_words{h}", tag=f"stage{h}", align_bytes=64) for h in range(2)]
+        gather_scales(0, 0, 0, J, first_scales[:])
+        for h in range(2):
+            gather_words(0, h, first_words[h][:])
+        for h in range(2):
+            part_words(0, h)
+        next_scales = keep.tile([P, J + 4 * JH], U8, name="next_scales", tag="stage0", align_bytes=64)
+        next_words = keep.tile([P, 2, 4 * JH], U8, name="next_words", tag="stage1", align_bytes=64)
+        gather_scales(0, 1, 0, J, next_scales[:, 0:J])
+        for g in (1, 2):
             for a in range(2):
-                for jt in range(4):
-                    for hb in range(2):
-                        first_layer(g, a, hb, jt)
+                c0 = J + JH * (2 * (g - 1) + a)
+                gather_scales(g, a, 0, JH, next_scales[:, c0 : c0 + JH])
+        for g in (1, 2):
+            gather_words(g, 0, next_words[:, g - 1, :])
+        for g in (1, 2):
+            part_words(g, 0)
+        for g in (1, 2):
+            cast_w2(0, g - 1, 0, HALF, False)
+            quantize_w2(0, g - 1)
+            last = keep.tile([P, 6 * JH], U8, name=f"last{g}", tag=f"grp0{g - 1}", align_bytes=64)
+            gather_words(g, 1, last[:, 0 : 4 * JH])
+            for a in range(2):
+                gather_scales(g, a, JH, J, last[:, (4 + a) * JH : (5 + a) * JH])
+            part_words(g, 1)
+
         for a in range(2):
             for jt in range(4):
-                first_layer(2, a, 0, jt)
-        cast_w2(1, 0, False)
+                for hb in range(2):
+                    first_layer(0, a, hb, jt)
+        for h in range(2):
+            for a in range(2):
+                for hb in range(2):
+                    for jt in (2 * h, 2 * h + 1):
+                        first_layer(1, a, hb, jt)
+            for a in range(2):
+                for jt in (2 * h, 2 * h + 1):
+                    first_layer(2, a, 0, jt)
+        cast_w2(1, 0, 0, HALF, False)
         quantize_w2(1, 0)
-        for jt in range(4):
+        cast_w2(1, 1, 0, HALF // 2, True)
+        for jt in range(2):
             silu(0, jt)
-        cast_w2(1, 1, True)
+        cast_w2(1, 1, HALF // 2, HALF, False)
+        quantize_w2(1, 1)
+        for jt in range(2, 4):
+            silu(0, jt)
         for jt in range(4):
             first_layer(2, 0, 1, jt)
-        quantize_w2(1, 1)
         for jt in range(4):
             turn(0, jt)
             smooth(0, jt)
+            if jt % 2 == 1:
+                quantize_h(0, jt - 1, jt + 1)
         for jt in range(4):
             first_layer(2, 1, 1, jt)
-            quantize_h(0, jt)
         for jt in range(4):
             silu(1, jt)
             turn(1, jt)
             smooth(1, jt)
-            quantize_h(1, jt)
+            quantize_h(1, jt, jt + 1)
             second_layer(jt)

@@ -20,6 +20,7 @@ MULT = mybir.AluOpType.mult
 P = 128
 HALF = 512
 JH = J // 2
+SCALES_AT = (3072, 0, 1536)
 
 
 def tile_list_rvq_silu_bias_kernel(
@@ -32,27 +33,27 @@ def tile_list_rvq_silu_bias_kernel(
 
         offsets = keep.tile([P, 3 * J // 16], U16, name="offsets")
         tabw = keep.tile([P, T], I32, name="tabw", align_bytes=64)
-        tabs = keep.tile([P, 2, T], U8, name="tabs", align_bytes=64)
+        tabs = keep.tile([P, T], U8, name="tabs", align_bytes=64)
+        picked = keep.tile([P, 3584], U8, name="picked", align_bytes=64)
+        moved = [keep.tile([P, J], U8, name=f"moved{g}", align_bytes=64) for g in range(3)]
         wdw = keep.tile([P, 2, 2 * N], U8, name="wdw", align_bytes=64)
         wds = keep.tile([P, 2, N], U8, name="wds", align_bytes=64)
-        w0w = keep.tile([P, 2, 2 * R], U8, name="w0w", align_bytes=64)
+        w0w = [keep.tile([P, 2 * R], U8, name=f"w0w{a}", align_bytes=64) for a in range(2)]
         w0s = keep.tile([P, 2, R], U8, name="w0s", align_bytes=64)
-        w1w = keep.tile([P, 2, 4 * R], U8, name="w1w", align_bytes=64)
+        w1w = [keep.tile([P, 2, 4 * HALF], U8, name=f"w1w{hb}", align_bytes=64) for hb in range(2)]
         w1s = keep.tile([P, 2, R], U8, name="w1s", align_bytes=64)
         smt = keep.tile([P, 2, 4], F32, name="smt")
         bias = keep.tile([P, 2], F32, name="bias")
         ident = keep.tile([P, P], F32, name="ident", align_bytes=64)
         warm = keep.tile([P, 2], F32, name="warm")
-        gw = {}
         vw = [keep.tile([P, 2, 2 * J], U8, name=f"vw{g}", align_bytes=64) for g in range(3)]
-        gs = {}
         raw = {}
+        staged = {}
         grp = {}
         w2c = {}
         w2s = {}
         for hb in range(2):
             for a in range(2):
-                raw[hb, a] = keep.tile([P, 4, HALF], F32, name=f"raw{hb}{a}", align_bytes=64)
                 grp[hb, a] = keep.tile([P, HALF, 4], BF16, name=f"grp{hb}{a}", tag=f"grp{hb}{a}", align_bytes=64)
                 w2c[hb, a] = keep.tile([P, HALF], U32, name=f"w2c{hb}{a}", align_bytes=64)
                 w2s[hb, a] = keep.tile([P, HALF], U8, name=f"w2s{hb}{a}", align_bytes=64)
@@ -64,39 +65,46 @@ def tile_list_rvq_silu_bias_kernel(
             for jt in range(4):
                 acc[hb, jt] = psum.tile([P, HALF], F32, name=f"acc{hb}{jt}", tag=f"bank{hb}{jt}")
 
-        def load_planes(plane, scales):
+        def load_planes(plane, scales, queue):
             for q in range(4):
-                nc.sync.dma_start(
+                queue.dma_start(
                     out=plane[32 * q : 32 * q + 4, :, :].bitcast(I32),
                     in_=scales[:, 4 * q : 4 * q + 4, :].bitcast(I32).rearrange("a r c -> r a c"),
                 )
 
-        def load_w2(hb, a):
-            rows = w2[HALF * a : HALF * (a + 1), HALF * hb : HALF * (hb + 1)]
-            nc.sync.dma_start(out=raw[hb, a][:], in_=rows.rearrange("(p i) c -> p i c", i=4))
+        def load_w2(hb, a, c0, c1):
+            raw[hb, a, c0] = keep.tile([P, 4, c1 - c0], F32, name=f"raw{hb}{a}{c0}", align_bytes=64)
+            rows = w2[HALF * a : HALF * (a + 1), HALF * hb + c0 : HALF * hb + c1]
+            nc.sync.dma_start(out=raw[hb, a, c0][:], in_=rows.rearrange("(p i) c -> p i c", i=4))
+
+        def load_w1(hb):
+            cols = w1_words[:, :, HALF * hb : HALF * (hb + 1), :]
+            nc.sync.dma_start(out=w1w[hb][:].bitcast(I32), in_=cols.rearrange("a p r i -> p a (r i)").bitcast(I32))
 
         def places(g, j0, j1):
             return offsets[:, (g * J + j0) // 16 : (g * J + j1) // 16]
 
-        def gather_scales(g, a, j0, j1, dst):
-            for jt in range(j0 // P, j1 // P):
-                gs[g, a, jt] = dst[:, P * jt - j0 : P * (jt + 1) - j0]
-            nc.vector.tensor_copy(out=dst, in_=tabs[:, a, :].indirect(places(g, j0, j1)))
+        def gather_scales(g, j0, j1):
+            dst = picked[:, SCALES_AT[g] + j0 : SCALES_AT[g] + j1]
+            nc.vector.tensor_copy(out=dst, in_=tabs[:].indirect(places(g, j0, j1)))
 
-        def gather_words(g, h, dst):
-            gw[g, h] = dst
-            lst = places(g, JH * h, JH * (h + 1))
-            nc.vector.tensor_copy(out=dst.bitcast(U32), in_=tabw[:].bitcast(U32).indirect(lst))
+        def move_scales(g, queue):
+            src = picked[4:116, SCALES_AT[g] : SCALES_AT[g] + J]
+            queue.dma_start(out=moved[g][0:112, :].bitcast(I32), in_=src.bitcast(I32))
 
-        def part_words(g, h):
+        def gather_words(g, j0, j1, at):
+            staged[g, j0] = picked[:, at : at + 4 * (j1 - j0)]
+            nc.vector.tensor_copy(out=staged[g, j0].bitcast(U32), in_=tabw[:].bitcast(U32).indirect(places(g, j0, j1)))
+
+        def part_words(g, j0, j1):
             nc.vector.tensor_copy(
-                out=vw[g][:, :, 2 * JH * h : 2 * JH * (h + 1)].bitcast(U16),
-                in_=gw[g, h].bitcast(U16).rearrange("p (j d) -> p d j", d=2),
+                out=vw[g][:, :, 2 * j0 : 2 * j1].bitcast(U16),
+                in_=staged[g, j0].bitcast(U16).rearrange("p (j d) -> p d j", d=2),
             )
 
         def cast_w2(hb, a, c0, c1, on_vector):
             dst = grp[hb, a][:, c0:c1, :].rearrange("p (c e) i -> p c i e", e=4)
-            src = raw[hb, a][:, :, c0:c1].rearrange("p i (c e) -> p c i e", e=4)
+            src = raw[hb, a, c0][:].rearrange("p i (c e) -> p c i e", e=4)
             if on_vector:
                 nc.vector.tensor_copy(out=dst, in_=src)
             else:
@@ -110,15 +118,19 @@ def tile_list_rvq_silu_bias_kernel(
         def first_layer(g, a, hb, jt):
             cols = slice(HALF * hb, HALF * (hb + 1))
             if g == 0:
-                rhs, rhs_scale = w0w[:, a, 2 * cols.start : 2 * cols.stop].bitcast(FP4X4), w0s[:, a, cols]
+                rhs, rhs_scale = w0w[a][:, 2 * cols.start : 2 * cols.stop].bitcast(FP4X4), w0s[:, a, cols]
             elif g == 1:
-                rhs, rhs_scale = w1w[:, a, 4 * cols.start : 4 * cols.stop].bitcast(FP8X4), w1s[:, a, cols]
+                rhs, rhs_scale = w1w[hb][:, a, :].bitcast(FP8X4), w1s[:, a, cols]
             else:
                 rhs, rhs_scale = w2c[hb, a][:].bitcast(FP8X4), w2s[hb, a][:]
+            if a == 0:
+                lhsT_scale = picked[:, SCALES_AT[g] + P * jt : SCALES_AT[g] + P * (jt + 1)]
+            else:
+                lhsT_scale = moved[g][:, P * jt : P * (jt + 1)]
             nc.tensor.matmul_mx(
                 out=acc[hb, jt][:],
                 lhsT=vw[g][:, a, 2 * P * jt : 2 * P * (jt + 1)].bitcast(FP4X4),
-                lhsT_scale=gs[g, a, jt],
+                lhsT_scale=lhsT_scale,
                 rhs=rhs,
                 rhs_scale=rhs_scale,
                 start=(g == 0 and a == 0),
@@ -176,90 +188,86 @@ def tile_list_rvq_silu_bias_kernel(
                 )
             nc.sync.dma_start(out=out.rearrange("(nt p) j -> p nt j", p=P)[:, :, cols], in_=res[:])
 
-        nc.vector.memset(tabs[:, 0, :].bitcast(I32), 0)
-        nc.gpsimd.memset(tabs[:, 1, :].bitcast(I32), 0)
-        nc.vector.memset(warm[:], 0.0)
+        nc.vector.memset(tabs[:].bitcast(I32), 0)
         nc.vector.memset(w0s[:].rearrange("p a c -> p (a c)").bitcast(I32), 0)
         nc.vector.memset(w1s[:].rearrange("p a c -> p (a c)").bitcast(I32), 0)
+        nc.vector.memset(warm[:], 0.0)
+        for g in range(3):
+            nc.vector.memset(moved[g][:].bitcast(I32), 0)
         nc.vector.memset(wds[:].rearrange("p a c -> p (a c)").bitcast(I32), 0)
         nc.scalar.activation(out=warm[:, 1:2], in_=warm[:, 0:1], func=ACT.Silu)
         make_identity(nc, ident[:])
 
         nc.sync.dma_start(offsets[:], offs)
-        load_planes(tabs, tab_scales)
+        for q in range(4):
+            nc.sync.dma_start(
+                out=tabs[32 * q : 32 * q + 8, :].bitcast(I32), in_=tab_scales[:, 4 * q : 4 * q + 4, :].bitcast(I32)
+            )
         nc.sync.dma_start(out=tabw[:], in_=tab_words[0].rearrange("p t f -> p (t f)").bitcast(I32))
-        nc.sync.dma_start(out=w0w[:, 0, :].bitcast(I32), in_=w0_words[0].bitcast(I32))
-        load_planes(w0s, w0_scales)
-        nc.sync.dma_start(out=w0w[:, 1, :].bitcast(I32), in_=w0_words[1].bitcast(I32))
-        load_w2(0, 0)
-        load_planes(w1s, w1_scales)
-        nc.sync.dma_start(out=w1w[:].bitcast(I32), in_=w1_words.rearrange("a p r i -> p a (r i)").bitcast(I32))
-        load_w2(0, 1)
-        load_w2(1, 0)
+        nc.sync.dma_start(out=w0w[0][:].bitcast(I32), in_=w0_words[0].bitcast(I32))
+        load_planes(w0s, w0_scales, nc.sync)
+        nc.sync.dma_start(out=w0w[1][:].bitcast(I32), in_=w0_words[1].bitcast(I32))
+        load_w2(0, 0, 0, JH)
+        load_w2(0, 0, JH, HALF)
+        gather_scales(0, 0, J)
+        move_scales(0, nc.sync)
+        load_w2(0, 1, 0, HALF)
+        gather_words(0, 0, P, 1280)
+        gather_words(0, P, JH, 0)
+        part_words(0, 0, P)
+        part_words(0, P, JH)
+        gather_words(0, JH, J, 1280)
+        gather_scales(1, 0, J)
+        move_scales(1, nc.sync)
+        load_planes(w1s, w1_scales, nc.sync)
+        load_w1(0)
+        part_words(0, JH, J)
+        gather_scales(2, 0, J)
+        move_scales(2, nc.sync)
+        load_w2(1, 0, 0, HALF)
         nc.sync.dma_start(out=smt[:], in_=sm.rearrange("(h p i) -> p h i", h=2, i=4))
-        load_w2(1, 1)
-        load_planes(wds, wd_scales)
+        load_w2(1, 1, 0, HALF)
+        load_w1(1)
+        load_planes(wds, wd_scales, nc.sync)
         nc.sync.dma_start(out=wdw[:].bitcast(I32), in_=wd_words.bitcast(I32).rearrange("a p c -> p a c"))
         with nc.allow_non_contiguous_dma(reason="one bias value to a partition"):
             nc.sync.dma_start(out=bias[:], in_=b.rearrange("(nt p) -> p nt", p=P))
+        for g in (1, 2):
+            gather_words(g, 0, JH, 512)
+            gather_words(g, JH, J, 2048)
+            part_words(g, 0, JH)
+            part_words(g, JH, J)
 
-        first_scales = keep.tile([P, J], U8, name="first_scales", align_bytes=64)
-        first_words = [keep.tile([P, 4 * JH], U8, name=f"first_words{h}", tag=f"stage{h}", align_bytes=64) for h in range(2)]
-        gather_scales(0, 0, 0, J, first_scales[:])
-        for h in range(2):
-            gather_words(0, h, first_words[h][:])
-        for h in range(2):
-            part_words(0, h)
-        next_scales = keep.tile([P, J + 4 * JH], U8, name="next_scales", tag="stage0", align_bytes=64)
-        next_words = keep.tile([P, 2, 4 * JH], U8, name="next_words", tag="stage1", align_bytes=64)
-        gather_scales(0, 1, 0, J, next_scales[:, 0:J])
-        for g in (1, 2):
-            for a in range(2):
-                c0 = J + JH * (2 * (g - 1) + a)
-                gather_scales(g, a, 0, JH, next_scales[:, c0 : c0 + JH])
-        for g in (1, 2):
-            gather_words(g, 0, next_words[:, g - 1, :])
-        for g in (1, 2):
-            part_words(g, 0)
-        for g in (1, 2):
-            cast_w2(0, g - 1, 0, HALF, False)
-            quantize_w2(0, g - 1)
-            last = keep.tile([P, 6 * JH], U8, name=f"last{g}", tag=f"grp0{g - 1}", align_bytes=64)
-            gather_words(g, 1, last[:, 0 : 4 * JH])
-            for a in range(2):
-                gather_scales(g, a, JH, J, last[:, (4 + a) * JH : (5 + a) * JH])
-            part_words(g, 1)
+        cast_w2(0, 0, 0, JH, False)
+        cast_w2(0, 0, JH, HALF, False)
+        quantize_w2(0, 0)
+        cast_w2(0, 1, 0, HALF, False)
+        quantize_w2(0, 1)
+        cast_w2(1, 0, 0, HALF, False)
+        quantize_w2(1, 0)
+        cast_w2(1, 1, 0, HALF, True)
+        quantize_w2(1, 1)
 
         for a in range(2):
             for jt in range(4):
                 for hb in range(2):
                     first_layer(0, a, hb, jt)
-        for h in range(2):
+        for g in (1, 2):
             for a in range(2):
-                for hb in range(2):
-                    for jt in (2 * h, 2 * h + 1):
-                        first_layer(1, a, hb, jt)
+                for jt in range(4):
+                    first_layer(g, a, 0, jt)
+        for jt in range(4):
+            silu(0, jt)
+        for a in range(2):
+            for jt in range(4):
+                first_layer(1, a, 1, jt)
+            for jt in (2 * a, 2 * a + 1):
+                turn(0, jt)
+                smooth(0, jt)
+            quantize_h(0, 2 * a, 2 * a + 2)
+        for jt in range(4):
             for a in range(2):
-                for jt in (2 * h, 2 * h + 1):
-                    first_layer(2, a, 0, jt)
-        cast_w2(1, 0, 0, HALF, False)
-        quantize_w2(1, 0)
-        cast_w2(1, 1, 0, HALF // 2, True)
-        for jt in range(2):
-            silu(0, jt)
-        cast_w2(1, 1, HALF // 2, HALF, False)
-        quantize_w2(1, 1)
-        for jt in range(2, 4):
-            silu(0, jt)
-        for jt in range(4):
-            first_layer(2, 0, 1, jt)
-        for jt in range(4):
-            turn(0, jt)
-            smooth(0, jt)
-            if jt % 2 == 1:
-                quantize_h(0, jt - 1, jt + 1)
-        for jt in range(4):
-            first_layer(2, 1, 1, jt)
+                first_layer(2, a, 1, jt)
         for jt in range(4):
             silu(1, jt)
             turn(1, jt)

@@ -57,7 +57,7 @@ def tile_list_rvq_silu_bias_kernel(
                 grp[hb, a] = keep.tile([P, HALF, 4], BF16, name=f"grp{hb}{a}", tag=f"grp{hb}{a}", align_bytes=64)
                 w2c[hb, a] = keep.tile([P, HALF], U32, name=f"w2c{hb}{a}", align_bytes=64)
                 w2s[hb, a] = keep.tile([P, HALF], U8, name=f"w2s{hb}{a}", align_bytes=64)
-        hgrp = [keep.tile([P, J, 4], BF16, name=f"hgrp{hb}", align_bytes=64) for hb in range(2)]
+        hgrp = {}
         hc = [keep.tile([P, J], U32, name=f"hc{hb}", align_bytes=64) for hb in range(2)]
         hs = [keep.tile([P, J], U8, name=f"hs{hb}", align_bytes=64) for hb in range(2)]
         acc = {}
@@ -73,7 +73,7 @@ def tile_list_rvq_silu_bias_kernel(
                 )
 
         def load_w2(hb, a, c0, c1):
-            raw[hb, a, c0] = keep.tile([P, 4, c1 - c0], F32, name=f"raw{hb}{a}{c0}", align_bytes=64)
+            raw[hb, a, c0] = keep.tile([P, 4, c1 - c0], F32, name=f"raw{hb}{a}{c0}", tag=f"raw{hb}{a}{c0}", align_bytes=64)
             rows = w2[HALF * a : HALF * (a + 1), HALF * hb + c0 : HALF * hb + c1]
             nc.sync.dma_start(out=raw[hb, a, c0][:], in_=rows.rearrange("(p i) c -> p i c", i=4))
 
@@ -196,7 +196,8 @@ def tile_list_rvq_silu_bias_kernel(
             nc.vector.memset(moved[g][:].bitcast(I32), 0)
         nc.vector.memset(wds[:].rearrange("p a c -> p (a c)").bitcast(I32), 0)
         nc.scalar.activation(out=warm[:, 1:2], in_=warm[:, 0:1], func=ACT.Silu)
-        make_identity(nc, ident[:])
+        nc.vector.memset(ident[:], 0.0)
+        make_identity(nc, ident[:], nomemset=True)
 
         nc.sync.dma_start(offsets[:], offs)
         for q in range(4):
@@ -207,10 +208,11 @@ def tile_list_rvq_silu_bias_kernel(
         nc.sync.dma_start(out=w0w[0][:].bitcast(I32), in_=w0_words[0].bitcast(I32))
         load_planes(w0s, w0_scales, nc.sync)
         nc.sync.dma_start(out=w0w[1][:].bitcast(I32), in_=w0_words[1].bitcast(I32))
-        load_w2(0, 0, 0, JH)
-        load_w2(0, 0, JH, HALF)
+        load_w2(0, 0, 0, HALF)
         gather_scales(0, 0, J)
         move_scales(0, nc.sync)
+        load_planes(w1s, w1_scales, nc.sync)
+        load_w1(0)
         load_w2(0, 1, 0, HALF)
         gather_words(0, 0, P, 1280)
         gather_words(0, P, JH, 0)
@@ -219,15 +221,14 @@ def tile_list_rvq_silu_bias_kernel(
         gather_words(0, JH, J, 1280)
         gather_scales(1, 0, J)
         move_scales(1, nc.sync)
-        load_planes(w1s, w1_scales, nc.sync)
-        load_w1(0)
+        load_w1(1)
         part_words(0, JH, J)
         gather_scales(2, 0, J)
-        move_scales(2, nc.sync)
         load_w2(1, 0, 0, HALF)
+        move_scales(2, nc.sync)
         nc.sync.dma_start(out=smt[:], in_=sm.rearrange("(h p i) -> p h i", h=2, i=4))
-        load_w2(1, 1, 0, HALF)
-        load_w1(1)
+        load_w2(1, 1, 0, JH)
+        load_w2(1, 1, JH, HALF)
         load_planes(wds, wd_scales, nc.sync)
         nc.sync.dma_start(out=wdw[:].bitcast(I32), in_=wd_words.bitcast(I32).rearrange("a p c -> p a c"))
         with nc.allow_non_contiguous_dma(reason="one bias value to a partition"):
@@ -238,37 +239,42 @@ def tile_list_rvq_silu_bias_kernel(
             part_words(g, 0, JH)
             part_words(g, JH, J)
 
-        cast_w2(0, 0, 0, JH, False)
-        cast_w2(0, 0, JH, HALF, False)
+        cast_w2(0, 0, 0, HALF, False)
         quantize_w2(0, 0)
         cast_w2(0, 1, 0, HALF, False)
         quantize_w2(0, 1)
         cast_w2(1, 0, 0, HALF, False)
         quantize_w2(1, 0)
-        cast_w2(1, 1, 0, HALF, True)
+        cast_w2(1, 1, 0, JH, False)
+        cast_w2(1, 1, JH, HALF, True)
         quantize_w2(1, 1)
+        hgrp[0] = keep.tile([P, J, 4], BF16, name="hgrp0", tag=f"raw11{JH}", align_bytes=64)
+        hgrp[1] = keep.tile([P, J, 4], BF16, name="hgrp1", align_bytes=64)
 
         for a in range(2):
             for jt in range(4):
                 for hb in range(2):
                     first_layer(0, a, hb, jt)
-        for g in (1, 2):
-            for a in range(2):
-                for jt in range(4):
-                    first_layer(g, a, 0, jt)
+        for a in range(2):
+            for jt in range(4):
+                first_layer(1, a, 0, jt)
         for jt in range(4):
+            first_layer(2, 0, 0, jt)
+        for jt in range(4):
+            first_layer(2, 1, 0, jt)
             silu(0, jt)
         for a in range(2):
             for jt in range(4):
                 first_layer(1, a, 1, jt)
-            for jt in (2 * a, 2 * a + 1):
-                turn(0, jt)
-                smooth(0, jt)
-            quantize_h(0, 2 * a, 2 * a + 2)
+        for jt in range(4):
+            turn(0, jt)
+        for jt in range(4):
+            smooth(0, jt)
+            if jt % 2 == 1:
+                quantize_h(0, jt - 1, jt + 1)
         for jt in range(4):
             for a in range(2):
                 first_layer(2, a, 1, jt)
-        for jt in range(4):
             silu(1, jt)
             turn(1, jt)
             smooth(1, jt)

@@ -20,7 +20,7 @@ MULT = mybir.AluOpType.mult
 P = 128
 HALF = 512
 JH = J // 2
-SCALES_AT = (3072, 0, 1536)
+SCALES_AT = (4096, 0, 1536)
 
 
 def tile_list_rvq_silu_bias_kernel(
@@ -34,19 +34,19 @@ def tile_list_rvq_silu_bias_kernel(
         offsets = keep.tile([P, 3 * J // 16], U16, name="offsets")
         tabw = keep.tile([P, T], I32, name="tabw", align_bytes=64)
         tabs = keep.tile([P, T], U8, name="tabs", align_bytes=64)
-        picked = keep.tile([P, 3584], U8, name="picked", align_bytes=64)
+        picked = keep.tile([P, 4608], U8, name="picked", align_bytes=64)
         moved = [keep.tile([P, J], U8, name=f"moved{g}", align_bytes=64) for g in range(3)]
         wdw = keep.tile([P, 2, 2 * N], U8, name="wdw", align_bytes=64)
         wds = keep.tile([P, 2, N], U8, name="wds", align_bytes=64)
         w0w = [keep.tile([P, 2 * R], U8, name=f"w0w{a}", align_bytes=64) for a in range(2)]
         w0s = keep.tile([P, 2, R], U8, name="w0s", align_bytes=64)
-        w1w = [keep.tile([P, 2, 4 * HALF], U8, name=f"w1w{hb}", align_bytes=64) for hb in range(2)]
+        w1w = {}
         w1s = keep.tile([P, 2, R], U8, name="w1s", align_bytes=64)
         smt = keep.tile([P, 2, 4], F32, name="smt")
         bias = keep.tile([P, 2], F32, name="bias")
         ident = keep.tile([P, P], F32, name="ident", align_bytes=64)
         warm = keep.tile([P, 2], F32, name="warm")
-        vw = [keep.tile([P, 2, 2 * J], U8, name=f"vw{g}", align_bytes=64) for g in range(3)]
+        vw = {g: keep.tile([P, 2, 2 * J], U8, name=f"vw{g}", align_bytes=64) for g in range(2)}
         raw = {}
         staged = {}
         grp = {}
@@ -77,9 +77,12 @@ def tile_list_rvq_silu_bias_kernel(
             rows = w2[HALF * a : HALF * (a + 1), HALF * hb + c0 : HALF * hb + c1]
             nc.sync.dma_start(out=raw[hb, a, c0][:], in_=rows.rearrange("(p i) c -> p i c", i=4))
 
-        def load_w1(hb):
-            cols = w1_words[:, :, HALF * hb : HALF * (hb + 1), :]
-            nc.sync.dma_start(out=w1w[hb][:].bitcast(I32), in_=cols.rearrange("a p r i -> p a (r i)").bitcast(I32))
+        def load_w1(hb, a0, a1):
+            tile = keep.tile([P, a1 - a0, 4 * HALF], U8, name=f"w1w{hb}{a0}", align_bytes=64)
+            for a in range(a0, a1):
+                w1w[hb, a] = tile[:, a - a0, :]
+            cols = w1_words[a0:a1, :, HALF * hb : HALF * (hb + 1), :]
+            nc.sync.dma_start(out=tile[:].bitcast(I32), in_=cols.rearrange("a p r i -> p a (r i)").bitcast(I32))
 
         def places(g, j0, j1):
             return offsets[:, (g * J + j0) // 16 : (g * J + j1) // 16]
@@ -110,17 +113,19 @@ def tile_list_rvq_silu_bias_kernel(
             else:
                 nc.scalar.copy(out=dst, in_=src)
 
-        def quantize_w2(hb, a):
+        def quantize_w2(hb, a, c0, c1):
             nc.vector.quantize_mx(
-                out=w2c[hb, a][:].bitcast(FP8X4), scales=w2s[hb, a][:], in_=grp[hb, a][:].rearrange("p c i -> p (c i)")
+                out=w2c[hb, a][:, c0:c1].bitcast(FP8X4),
+                scales=w2s[hb, a][:, c0:c1],
+                in_=grp[hb, a][:, c0:c1, :].rearrange("p c i -> p (c i)"),
             )
 
-        def first_layer(g, a, hb, jt):
+        def first_layer(g, a, hb, jt, last=False):
             cols = slice(HALF * hb, HALF * (hb + 1))
             if g == 0:
                 rhs, rhs_scale = w0w[a][:, 2 * cols.start : 2 * cols.stop].bitcast(FP4X4), w0s[:, a, cols]
             elif g == 1:
-                rhs, rhs_scale = w1w[hb][:, a, :].bitcast(FP8X4), w1s[:, a, cols]
+                rhs, rhs_scale = w1w[hb, a].bitcast(FP8X4), w1s[:, a, cols]
             else:
                 rhs, rhs_scale = w2c[hb, a][:].bitcast(FP8X4), w2s[hb, a][:]
             if a == 0:
@@ -134,7 +139,7 @@ def tile_list_rvq_silu_bias_kernel(
                 rhs=rhs,
                 rhs_scale=rhs_scale,
                 start=(g == 0 and a == 0),
-                stop=(g == 2 and a == 1),
+                stop=last,
             )
 
         act = {}
@@ -167,24 +172,29 @@ def tile_list_rvq_silu_bias_kernel(
                 in_=hgrp[hb][:, cols, :].rearrange("p j i -> p (j i)"),
             )
 
-        def second_layer(jt):
+        y = {}
+
+        def second_layer(hb, jt):
             cols = slice(P * jt, P * (jt + 1))
-            y = psum.tile([P, 2, P], F32, name=f"y{jt}", tag=f"bank0{jt}")
+            if hb == 0:
+                y[jt] = psum.tile([P, 2, P], F32, name=f"y{jt}", tag=f"bank1{jt}")
+            for nt in range(2):
+                nc.tensor.matmul_mx(
+                    out=y[jt][:, nt, :],
+                    lhsT=wdw[:, hb, 2 * P * nt : 2 * P * (nt + 1)].bitcast(FP4X4),
+                    lhsT_scale=wds[:, hb, P * nt : P * (nt + 1)],
+                    rhs=hc[hb][:, cols].bitcast(FP8X4),
+                    rhs_scale=hs[hb][:, cols],
+                    start=(hb == 0 and nt == 0),
+                    stop=(hb == 1 and nt == 1),
+                )
+
+        def store(jt):
+            cols = slice(P * jt, P * (jt + 1))
             res = keep.tile([P, 2, P], F32, name=f"res{jt}")
             for nt in range(2):
-                for hb in range(2):
-                    nc.tensor.matmul_mx(
-                        out=y[:, nt, :],
-                        lhsT=wdw[:, hb, 2 * P * nt : 2 * P * (nt + 1)].bitcast(FP4X4),
-                        lhsT_scale=wds[:, hb, P * nt : P * (nt + 1)],
-                        rhs=hc[hb][:, cols].bitcast(FP8X4),
-                        rhs_scale=hs[hb][:, cols],
-                        start=(hb == 0),
-                        stop=(hb == 1),
-                    )
-            for nt in range(2):
                 nc.scalar.activation(
-                    out=res[:, nt, :], in_=y[:, nt, :], func=ACT.Identity, bias=bias[:, nt : nt + 1]
+                    out=res[:, nt, :], in_=y[jt][:, nt, :], func=ACT.Identity, bias=bias[:, nt : nt + 1]
                 )
             nc.sync.dma_start(out=out.rearrange("(nt p) j -> p nt j", p=P)[:, :, cols], in_=res[:])
 
@@ -200,20 +210,20 @@ def tile_list_rvq_silu_bias_kernel(
         make_identity(nc, ident[:], nomemset=True)
 
         nc.sync.dma_start(offsets[:], offs)
+        nc.sync.dma_start(out=w0w[0][:].bitcast(I32), in_=w0_words[0].bitcast(I32))
         for q in range(4):
             nc.sync.dma_start(
                 out=tabs[32 * q : 32 * q + 8, :].bitcast(I32), in_=tab_scales[:, 4 * q : 4 * q + 4, :].bitcast(I32)
             )
         nc.sync.dma_start(out=tabw[:], in_=tab_words[0].rearrange("p t f -> p (t f)").bitcast(I32))
-        nc.sync.dma_start(out=w0w[0][:].bitcast(I32), in_=w0_words[0].bitcast(I32))
-        load_planes(w0s, w0_scales, nc.sync)
         nc.sync.dma_start(out=w0w[1][:].bitcast(I32), in_=w0_words[1].bitcast(I32))
+        load_planes(w0s, w0_scales, nc.sync)
         load_w2(0, 0, 0, HALF)
         gather_scales(0, 0, J)
         move_scales(0, nc.sync)
-        load_planes(w1s, w1_scales, nc.sync)
-        load_w1(0)
         load_w2(0, 1, 0, HALF)
+        load_planes(w1s, w1_scales, nc.sync)
+        load_w1(0, 0, 2)
         gather_words(0, 0, P, 1280)
         gather_words(0, P, JH, 0)
         part_words(0, 0, P)
@@ -221,33 +231,35 @@ def tile_list_rvq_silu_bias_kernel(
         gather_words(0, JH, J, 1280)
         gather_scales(1, 0, J)
         move_scales(1, nc.sync)
-        load_w1(1)
+        load_w1(1, 0, 1)
         part_words(0, JH, J)
+        gather_words(1, 0, J, 2048)
         gather_scales(2, 0, J)
         load_w2(1, 0, 0, HALF)
         move_scales(2, nc.sync)
         nc.sync.dma_start(out=smt[:], in_=sm.rearrange("(h p i) -> p h i", h=2, i=4))
         load_w2(1, 1, 0, JH)
         load_w2(1, 1, JH, HALF)
+        load_w1(1, 1, 2)
         load_planes(wds, wd_scales, nc.sync)
         nc.sync.dma_start(out=wdw[:].bitcast(I32), in_=wd_words.bitcast(I32).rearrange("a p c -> p a c"))
         with nc.allow_non_contiguous_dma(reason="one bias value to a partition"):
             nc.sync.dma_start(out=bias[:], in_=b.rearrange("(nt p) -> p nt", p=P))
-        for g in (1, 2):
-            gather_words(g, 0, JH, 512)
-            gather_words(g, JH, J, 2048)
-            part_words(g, 0, JH)
-            part_words(g, JH, J)
+        part_words(1, 0, J)
+        gather_words(2, 0, J, 2048)
 
         cast_w2(0, 0, 0, HALF, False)
-        quantize_w2(0, 0)
+        quantize_w2(0, 0, 0, HALF)
+        vw[2] = keep.tile([P, 2, 2 * J], U8, name="vw2", tag="grp00", align_bytes=64)
+        part_words(2, 0, J)
         cast_w2(0, 1, 0, HALF, False)
-        quantize_w2(0, 1)
+        quantize_w2(0, 1, 0, HALF)
         cast_w2(1, 0, 0, HALF, False)
-        quantize_w2(1, 0)
-        cast_w2(1, 1, 0, JH, False)
+        quantize_w2(1, 0, 0, HALF)
+        cast_w2(1, 1, 0, JH, True)
+        quantize_w2(1, 1, 0, JH)
         cast_w2(1, 1, JH, HALF, True)
-        quantize_w2(1, 1)
+        quantize_w2(1, 1, JH, HALF)
         hgrp[0] = keep.tile([P, J, 4], BF16, name="hgrp0", tag=f"raw11{JH}", align_bytes=64)
         hgrp[1] = keep.tile([P, J, 4], BF16, name="hgrp1", align_bytes=64)
 
@@ -259,13 +271,14 @@ def tile_list_rvq_silu_bias_kernel(
             for jt in range(4):
                 first_layer(1, a, 0, jt)
         for jt in range(4):
+            first_layer(1, 0, 1, jt)
+        for jt in range(4):
             first_layer(2, 0, 0, jt)
         for jt in range(4):
-            first_layer(2, 1, 0, jt)
+            first_layer(2, 1, 0, jt, last=True)
             silu(0, jt)
-        for a in range(2):
-            for jt in range(4):
-                first_layer(1, a, 1, jt)
+        for jt in range(4):
+            first_layer(2, 0, 1, jt)
         for jt in range(4):
             turn(0, jt)
         for jt in range(4):
@@ -273,10 +286,14 @@ def tile_list_rvq_silu_bias_kernel(
             if jt % 2 == 1:
                 quantize_h(0, jt - 1, jt + 1)
         for jt in range(4):
-            for a in range(2):
-                first_layer(2, a, 1, jt)
+            first_layer(1, 1, 1, jt)
+            first_layer(2, 1, 1, jt, last=True)
             silu(1, jt)
+        for jt in range(4):
             turn(1, jt)
+        for jt in range(4):
             smooth(1, jt)
+            second_layer(0, jt)
             quantize_h(1, jt, jt + 1)
-            second_layer(jt)
+            second_layer(1, jt)
+            store(jt)

@@ -45,7 +45,6 @@ def tile_list_rvq_silu_bias_kernel(
         smt = keep.tile([P, 2, 4], F32, name="smt")
         bias = keep.tile([P, 2], F32, name="bias")
         ident = keep.tile([P, P], F32, name="ident", align_bytes=64)
-        warm = keep.tile([P, 2], F32, name="warm")
         vw = {g: keep.tile([P, 2, 2 * J], U8, name=f"vw{g}", align_bytes=64) for g in range(2)}
         raw = {}
         staged = {}
@@ -54,7 +53,6 @@ def tile_list_rvq_silu_bias_kernel(
         w2s = {}
         for hb in range(2):
             for a in range(2):
-                grp[hb, a] = keep.tile([P, HALF, 4], BF16, name=f"grp{hb}{a}", tag=f"grp{hb}{a}", align_bytes=64)
                 w2c[hb, a] = keep.tile([P, HALF], U32, name=f"w2c{hb}{a}", align_bytes=64)
                 w2s[hb, a] = keep.tile([P, HALF], U8, name=f"w2s{hb}{a}", align_bytes=64)
         hgrp = {}
@@ -66,10 +64,10 @@ def tile_list_rvq_silu_bias_kernel(
                 acc[hb, jt] = psum.tile([P, HALF], F32, name=f"acc{hb}{jt}", tag=f"bank{hb}{jt}")
 
         def load_planes(plane, scales, queue):
-            for q in range(4):
+            for r in range(4):
                 queue.dma_start(
-                    out=plane[32 * q : 32 * q + 4, :, :].bitcast(I32),
-                    in_=scales[:, 4 * q : 4 * q + 4, :].bitcast(I32).rearrange("a r c -> r a c"),
+                    out=plane[r:P:32, :, :].bitcast(I32),
+                    in_=scales[:, r:16:4, :].bitcast(I32).rearrange("a q c -> q a c"),
                 )
 
         def load_w2(hb, a, c0, c1):
@@ -77,12 +75,12 @@ def tile_list_rvq_silu_bias_kernel(
             rows = w2[HALF * a : HALF * (a + 1), HALF * hb + c0 : HALF * hb + c1]
             nc.sync.dma_start(out=raw[hb, a, c0][:], in_=rows.rearrange("(p i) c -> p i c", i=4))
 
-        def load_w1(hb, a0, a1):
-            tile = keep.tile([P, a1 - a0, 4 * HALF], U8, name=f"w1w{hb}{a0}", align_bytes=64)
-            for a in range(a0, a1):
-                w1w[hb, a] = tile[:, a - a0, :]
-            cols = w1_words[a0:a1, :, HALF * hb : HALF * (hb + 1), :]
-            nc.sync.dma_start(out=tile[:].bitcast(I32), in_=cols.rearrange("a p r i -> p a (r i)").bitcast(I32))
+        def load_w1(a, hb0, hb1):
+            words = keep.tile([P, 4 * HALF * (hb1 - hb0)], U8, name=f"w1w{a}{hb0}", align_bytes=64)
+            for hb in range(hb0, hb1):
+                w1w[hb, a] = words[:, 4 * HALF * (hb - hb0) : 4 * HALF * (hb - hb0 + 1)]
+            cols = w1_words[a, :, HALF * hb0 : HALF * hb1, :]
+            nc.sync.dma_start(out=words[:].bitcast(I32), in_=cols.rearrange("p r i -> p (r i)").bitcast(I32))
 
         def places(g, j0, j1):
             return offsets[:, (g * J + j0) // 16 : (g * J + j1) // 16]
@@ -106,7 +104,8 @@ def tile_list_rvq_silu_bias_kernel(
             )
 
         def cast_w2(hb, a, c0, c1, on_vector):
-            dst = grp[hb, a][:, c0:c1, :].rearrange("p (c e) i -> p c i e", e=4)
+            grp[hb, a, c0] = keep.tile([P, c1 - c0, 4], BF16, name=f"grp{hb}{a}{c0}", tag=f"grp{hb}{a}{c0}", align_bytes=64)
+            dst = grp[hb, a, c0][:].rearrange("p (c e) i -> p c i e", e=4)
             src = raw[hb, a, c0][:].rearrange("p i (c e) -> p c i e", e=4)
             if on_vector:
                 nc.vector.tensor_copy(out=dst, in_=src)
@@ -117,7 +116,7 @@ def tile_list_rvq_silu_bias_kernel(
             nc.vector.quantize_mx(
                 out=w2c[hb, a][:, c0:c1].bitcast(FP8X4),
                 scales=w2s[hb, a][:, c0:c1],
-                in_=grp[hb, a][:, c0:c1, :].rearrange("p c i -> p (c i)"),
+                in_=grp[hb, a, c0][:].rearrange("p c i -> p (c i)"),
             )
 
         def first_layer(g, a, hb, jt, last=False):
@@ -158,7 +157,7 @@ def tile_list_rvq_silu_bias_kernel(
 
         def smooth(hb, jt):
             nc.vector.tensor_tensor(
-                out=hgrp[hb][:, P * jt : P * (jt + 1), :],
+                out=hgrp[hb, jt // 2][:, P * (jt % 2) : P * (jt % 2 + 1), :],
                 in0=turned[hb, jt][:].rearrange("p i j -> p j i"),
                 in1=smt[:, hb, :].unsqueeze(1).to_broadcast([P, P, 4]),
                 op=MULT,
@@ -169,7 +168,7 @@ def tile_list_rvq_silu_bias_kernel(
             nc.vector.quantize_mx(
                 out=hc[hb][:, cols].bitcast(FP8X4),
                 scales=hs[hb][:, cols],
-                in_=hgrp[hb][:, cols, :].rearrange("p j i -> p (j i)"),
+                in_=hgrp[hb, jt0 // 2][:, P * (jt0 % 2) : P * (jt0 % 2 + jt1 - jt0), :].rearrange("p j i -> p (j i)"),
             )
 
         y = {}
@@ -201,11 +200,9 @@ def tile_list_rvq_silu_bias_kernel(
         nc.vector.memset(tabs[:].bitcast(I32), 0)
         nc.vector.memset(w0s[:].rearrange("p a c -> p (a c)").bitcast(I32), 0)
         nc.vector.memset(w1s[:].rearrange("p a c -> p (a c)").bitcast(I32), 0)
-        nc.vector.memset(warm[:], 0.0)
         for g in range(3):
             nc.vector.memset(moved[g][:].bitcast(I32), 0)
         nc.vector.memset(wds[:].rearrange("p a c -> p (a c)").bitcast(I32), 0)
-        nc.scalar.activation(out=warm[:, 1:2], in_=warm[:, 0:1], func=ACT.Silu)
         nc.vector.memset(ident[:], 0.0)
         make_identity(nc, ident[:], nomemset=True)
 
@@ -221,9 +218,9 @@ def tile_list_rvq_silu_bias_kernel(
         load_w2(0, 0, 0, HALF)
         gather_scales(0, 0, J)
         move_scales(0, nc.sync)
-        load_w2(0, 1, 0, HALF)
         load_planes(w1s, w1_scales, nc.sync)
         load_w1(0, 0, 2)
+        load_w2(0, 1, 0, HALF)
         gather_words(0, 0, P, 1280)
         gather_words(0, P, JH, 0)
         part_words(0, 0, P)
@@ -237,10 +234,10 @@ def tile_list_rvq_silu_bias_kernel(
         gather_scales(2, 0, J)
         load_w2(1, 0, 0, HALF)
         move_scales(2, nc.sync)
+        load_w1(1, 1, 2)
         nc.sync.dma_start(out=smt[:], in_=sm.rearrange("(h p i) -> p h i", h=2, i=4))
         load_w2(1, 1, 0, JH)
         load_w2(1, 1, JH, HALF)
-        load_w1(1, 1, 2)
         load_planes(wds, wd_scales, nc.sync)
         nc.sync.dma_start(out=wdw[:].bitcast(I32), in_=wd_words.bitcast(I32).rearrange("a p c -> p a c"))
         with nc.allow_non_contiguous_dma(reason="one bias value to a partition"):
@@ -250,35 +247,37 @@ def tile_list_rvq_silu_bias_kernel(
 
         cast_w2(0, 0, 0, HALF, False)
         quantize_w2(0, 0, 0, HALF)
-        vw[2] = keep.tile([P, 2, 2 * J], U8, name="vw2", tag="grp00", align_bytes=64)
+        vw[2] = keep.tile([P, 2, 2 * J], U8, name="vw2", tag="grp000", align_bytes=64)
         part_words(2, 0, J)
         cast_w2(0, 1, 0, HALF, False)
         quantize_w2(0, 1, 0, HALF)
-        cast_w2(1, 0, 0, HALF, False)
+        cast_w2(1, 0, 0, HALF, True)
         quantize_w2(1, 0, 0, HALF)
         cast_w2(1, 1, 0, JH, True)
         quantize_w2(1, 1, 0, JH)
-        cast_w2(1, 1, JH, HALF, True)
-        quantize_w2(1, 1, JH, HALF)
-        hgrp[0] = keep.tile([P, J, 4], BF16, name="hgrp0", tag=f"raw11{JH}", align_bytes=64)
-        hgrp[1] = keep.tile([P, J, 4], BF16, name="hgrp1", align_bytes=64)
+        hgrp[0, 0] = keep.tile([P, JH, 4], BF16, name="hgrp00", tag="raw110", align_bytes=64)
+        hgrp[1, 0] = keep.tile([P, JH, 4], BF16, name="hgrp10", align_bytes=64)
+        hgrp[1, 1] = keep.tile([P, JH, 4], BF16, name="hgrp11", align_bytes=64)
 
         for a in range(2):
             for jt in range(4):
                 for hb in range(2):
                     first_layer(0, a, hb, jt)
-        for a in range(2):
+        for hb in range(2):
             for jt in range(4):
-                first_layer(1, a, 0, jt)
+                first_layer(1, 0, hb, jt)
         for jt in range(4):
-            first_layer(1, 0, 1, jt)
+            first_layer(1, 1, 0, jt)
         for jt in range(4):
             first_layer(2, 0, 0, jt)
         for jt in range(4):
             first_layer(2, 1, 0, jt, last=True)
             silu(0, jt)
+        cast_w2(1, 1, JH, HALF, False)
+        quantize_w2(1, 1, JH, HALF)
+        hgrp[0, 1] = keep.tile([P, JH, 4], BF16, name="hgrp01", tag=f"grp11{JH}", align_bytes=64)
         for jt in range(4):
-            first_layer(2, 0, 1, jt)
+            first_layer(1, 1, 1, jt)
         for jt in range(4):
             turn(0, jt)
         for jt in range(4):
@@ -286,7 +285,7 @@ def tile_list_rvq_silu_bias_kernel(
             if jt % 2 == 1:
                 quantize_h(0, jt - 1, jt + 1)
         for jt in range(4):
-            first_layer(1, 1, 1, jt)
+            first_layer(2, 0, 1, jt)
             first_layer(2, 1, 1, jt, last=True)
             silu(1, jt)
         for jt in range(4):

@@ -20,7 +20,7 @@ MULT = mybir.AluOpType.mult
 P = 128
 HALF = 512
 JH = J // 2
-SCALES_AT = (4096, 0, 1536)
+SCALES_AT = (4096, 0, 512)
 
 
 def tile_list_rvq_silu_bias_kernel(
@@ -35,7 +35,8 @@ def tile_list_rvq_silu_bias_kernel(
         tabw = keep.tile([P, T], I32, name="tabw", align_bytes=64)
         tabs = keep.tile([P, T], U8, name="tabs", align_bytes=64)
         picked = keep.tile([P, 4608], U8, name="picked", align_bytes=64)
-        moved = [keep.tile([P, J], U8, name=f"moved{g}", align_bytes=64) for g in range(3)]
+        moved = keep.tile([P, 3 * J], U8, name="moved", align_bytes=64)
+        warm = keep.tile([P, 2, 8], F32, name="warm")
         wdw = keep.tile([P, 2, 2 * N], U8, name="wdw", align_bytes=64)
         wds = keep.tile([P, 2, N], U8, name="wds", align_bytes=64)
         w0w = [keep.tile([P, 2 * R], U8, name=f"w0w{a}", align_bytes=64) for a in range(2)]
@@ -89,9 +90,9 @@ def tile_list_rvq_silu_bias_kernel(
             dst = picked[:, SCALES_AT[g] + j0 : SCALES_AT[g] + j1]
             nc.vector.tensor_copy(out=dst, in_=tabs[:].indirect(places(g, j0, j1)))
 
-        def move_scales(g, queue):
-            src = picked[4:116, SCALES_AT[g] : SCALES_AT[g] + J]
-            queue.dma_start(out=moved[g][0:112, :].bitcast(I32), in_=src.bitcast(I32))
+        def move_scales(g0, g1):
+            src = picked[16:128, SCALES_AT[g0] : SCALES_AT[g0] + J * (g1 - g0)]
+            nc.sync.dma_start(out=moved[0:112, J * g0 : J * g1].bitcast(I32), in_=src.bitcast(I32))
 
         def gather_words(g, j0, j1, at):
             staged[g, j0] = picked[:, at : at + 4 * (j1 - j0)]
@@ -130,7 +131,7 @@ def tile_list_rvq_silu_bias_kernel(
             if a == 0:
                 lhsT_scale = picked[:, SCALES_AT[g] + P * jt : SCALES_AT[g] + P * (jt + 1)]
             else:
-                lhsT_scale = moved[g][:, P * jt : P * (jt + 1)]
+                lhsT_scale = moved[:, J * g + P * jt : J * g + P * (jt + 1)]
             nc.tensor.matmul_mx(
                 out=acc[hb, jt][:],
                 lhsT=vw[g][:, a, 2 * P * jt : 2 * P * (jt + 1)].bitcast(FP4X4),
@@ -197,53 +198,54 @@ def tile_list_rvq_silu_bias_kernel(
                 )
             nc.sync.dma_start(out=out.rearrange("(nt p) j -> p nt j", p=P)[:, :, cols], in_=res[:])
 
-        nc.vector.memset(tabs[:].bitcast(I32), 0)
+        nc.gpsimd.memset(tabs[:].bitcast(I32), 0)
         nc.vector.memset(w0s[:].rearrange("p a c -> p (a c)").bitcast(I32), 0)
         nc.vector.memset(w1s[:].rearrange("p a c -> p (a c)").bitcast(I32), 0)
-        for g in range(3):
-            nc.vector.memset(moved[g][:].bitcast(I32), 0)
         nc.vector.memset(wds[:].rearrange("p a c -> p (a c)").bitcast(I32), 0)
+        nc.vector.memset(moved[:].bitcast(I32), 0)
         nc.vector.memset(ident[:], 0.0)
+        nc.vector.memset(warm[:, 0, :], 0.0)
+        nc.scalar.dma_start(out=smt[:], in_=sm.rearrange("(h p i) -> p h i", h=2, i=4))
+        nc.scalar.activation(out=warm[:, 1, 0:1], in_=warm[:, 0, 0:1], func=ACT.Silu)
+        load_planes(w1s, w1_scales, nc.gpsimd)
         make_identity(nc, ident[:], nomemset=True)
 
         nc.sync.dma_start(offsets[:], offs)
-        nc.sync.dma_start(out=w0w[0][:].bitcast(I32), in_=w0_words[0].bitcast(I32))
-        for q in range(4):
+        for r in range(4):
             nc.sync.dma_start(
-                out=tabs[32 * q : 32 * q + 8, :].bitcast(I32), in_=tab_scales[:, 4 * q : 4 * q + 4, :].bitcast(I32)
+                out=tabs[r:P:16, :].bitcast(I32),
+                in_=tab_scales[:, r:16:4, :].bitcast(I32).rearrange("a q c -> q a c"),
             )
         nc.sync.dma_start(out=tabw[:], in_=tab_words[0].rearrange("p t f -> p (t f)").bitcast(I32))
-        nc.sync.dma_start(out=w0w[1][:].bitcast(I32), in_=w0_words[1].bitcast(I32))
+        nc.sync.dma_start(out=w0w[0][:].bitcast(I32), in_=w0_words[0].bitcast(I32))
         load_planes(w0s, w0_scales, nc.sync)
+        nc.sync.dma_start(out=w0w[1][:].bitcast(I32), in_=w0_words[1].bitcast(I32))
         load_w2(0, 0, 0, HALF)
         gather_scales(0, 0, J)
-        move_scales(0, nc.sync)
-        load_planes(w1s, w1_scales, nc.sync)
+        move_scales(0, 1)
         load_w1(0, 0, 2)
         load_w2(0, 1, 0, HALF)
         gather_words(0, 0, P, 1280)
         gather_words(0, P, JH, 0)
         part_words(0, 0, P)
         part_words(0, P, JH)
-        gather_words(0, JH, J, 1280)
+        gather_words(0, JH, J, 768)
         gather_scales(1, 0, J)
-        move_scales(1, nc.sync)
         load_w1(1, 0, 1)
         part_words(0, JH, J)
-        gather_words(1, 0, J, 2048)
+        gather_words(1, 0, J, 1536)
         gather_scales(2, 0, J)
+        move_scales(1, 3)
         load_w2(1, 0, 0, HALF)
-        move_scales(2, nc.sync)
         load_w1(1, 1, 2)
-        nc.sync.dma_start(out=smt[:], in_=sm.rearrange("(h p i) -> p h i", h=2, i=4))
         load_w2(1, 1, 0, JH)
         load_w2(1, 1, JH, HALF)
-        load_planes(wds, wd_scales, nc.sync)
         nc.sync.dma_start(out=wdw[:].bitcast(I32), in_=wd_words.bitcast(I32).rearrange("a p c -> p a c"))
+        load_planes(wds, wd_scales, nc.sync)
         with nc.allow_non_contiguous_dma(reason="one bias value to a partition"):
             nc.sync.dma_start(out=bias[:], in_=b.rearrange("(nt p) -> p nt", p=P))
         part_words(1, 0, J)
-        gather_words(2, 0, J, 2048)
+        gather_words(2, 0, J, 1536)
 
         cast_w2(0, 0, 0, HALF, False)
         quantize_w2(0, 0, 0, HALF)

@@ -104,14 +104,15 @@ def tile_list_rvq_silu_bias_kernel(
                 in_=staged[g, j0].bitcast(U16).rearrange("p (j d) -> p d j", d=2),
             )
 
-        def cast_w2(hb, a, c0, c1, on_vector):
+        def cast_w2(hb, a, c0, c1, on_scalar):
             grp[hb, a, c0] = keep.tile([P, c1 - c0, 4], BF16, name=f"grp{hb}{a}{c0}", tag=f"grp{hb}{a}{c0}", align_bytes=64)
             dst = grp[hb, a, c0][:].rearrange("p (c e) i -> p c i e", e=4)
             src = raw[hb, a, c0][:].rearrange("p i (c e) -> p c i e", e=4)
-            if on_vector:
-                nc.vector.tensor_copy(out=dst, in_=src)
-            else:
-                nc.scalar.copy(out=dst, in_=src)
+            cut = on_scalar // 4
+            if cut > 0:
+                nc.scalar.copy(out=dst[:, :cut], in_=src[:, :cut])
+            if cut < (c1 - c0) // 4:
+                nc.vector.tensor_copy(out=dst[:, cut:], in_=src[:, cut:])
 
         def quantize_w2(hb, a, c0, c1):
             nc.vector.quantize_mx(
@@ -207,7 +208,6 @@ def tile_list_rvq_silu_bias_kernel(
         nc.vector.memset(warm[:, 0, :], 0.0)
         nc.scalar.dma_start(out=smt[:], in_=sm.rearrange("(h p i) -> p h i", h=2, i=4))
         nc.scalar.activation(out=warm[:, 1, 0:1], in_=warm[:, 0, 0:1], func=ACT.Silu)
-        load_planes(w1s, w1_scales, nc.gpsimd)
         make_identity(nc, ident[:], nomemset=True)
 
         nc.sync.dma_start(offsets[:], offs)
@@ -223,6 +223,7 @@ def tile_list_rvq_silu_bias_kernel(
         load_w2(0, 0, 0, HALF)
         gather_scales(0, 0, J)
         move_scales(0, 1)
+        load_planes(w1s, w1_scales, nc.sync)
         load_w1(0, 0, 2)
         load_w2(0, 1, 0, HALF)
         gather_words(0, 0, P, 1280)
@@ -247,19 +248,16 @@ def tile_list_rvq_silu_bias_kernel(
         part_words(1, 0, J)
         gather_words(2, 0, J, 1536)
 
-        cast_w2(0, 0, 0, HALF, False)
+        cast_w2(0, 0, 0, HALF, HALF)
         quantize_w2(0, 0, 0, HALF)
         vw[2] = keep.tile([P, 2, 2 * J], U8, name="vw2", tag="grp000", align_bytes=64)
         part_words(2, 0, J)
-        cast_w2(0, 1, 0, HALF, False)
+        cast_w2(0, 1, 0, HALF, 320)
         quantize_w2(0, 1, 0, HALF)
-        cast_w2(1, 0, 0, HALF, True)
+        cast_w2(1, 0, 0, HALF, 0)
         quantize_w2(1, 0, 0, HALF)
-        cast_w2(1, 1, 0, JH, True)
+        cast_w2(1, 1, 0, JH, 0)
         quantize_w2(1, 1, 0, JH)
-        hgrp[0, 0] = keep.tile([P, JH, 4], BF16, name="hgrp00", tag="raw110", align_bytes=64)
-        hgrp[1, 0] = keep.tile([P, JH, 4], BF16, name="hgrp10", align_bytes=64)
-        hgrp[1, 1] = keep.tile([P, JH, 4], BF16, name="hgrp11", align_bytes=64)
 
         for a in range(2):
             for jt in range(4):
@@ -275,26 +273,31 @@ def tile_list_rvq_silu_bias_kernel(
         for jt in range(4):
             first_layer(2, 1, 0, jt, last=True)
             silu(0, jt)
-        cast_w2(1, 1, JH, HALF, False)
+        cast_w2(1, 1, JH, HALF, 128)
         quantize_w2(1, 1, JH, HALF)
-        hgrp[0, 1] = keep.tile([P, JH, 4], BF16, name="hgrp01", tag=f"grp11{JH}", align_bytes=64)
+        hgrp[0, 0] = keep.tile([P, JH, 4], BF16, name="hgrp00", tag=f"grp11{JH}", align_bytes=64)
+        hgrp[0, 1] = keep.tile([P, JH, 4], BF16, name="hgrp01", tag=f"raw11{JH}", align_bytes=64)
+        hgrp[1, 0] = keep.tile([P, JH, 4], BF16, name="hgrp10", align_bytes=64)
+        hgrp[1, 1] = keep.tile([P, JH, 4], BF16, name="hgrp11", align_bytes=64)
         for jt in range(4):
             first_layer(1, 1, 1, jt)
         for jt in range(4):
             turn(0, jt)
         for jt in range(4):
+            first_layer(2, 0, 1, jt)
+        for jt in range(4):
+            first_layer(2, 1, 1, jt, last=True)
+            silu(1, jt)
+        for jt in range(4):
             smooth(0, jt)
             if jt % 2 == 1:
                 quantize_h(0, jt - 1, jt + 1)
         for jt in range(4):
-            first_layer(2, 0, 1, jt)
-            first_layer(2, 1, 1, jt, last=True)
-            silu(1, jt)
-        for jt in range(4):
             turn(1, jt)
         for jt in range(4):
             smooth(1, jt)
-            second_layer(0, jt)
             quantize_h(1, jt, jt + 1)
+        for jt in range(4):
+            second_layer(0, jt)
             second_layer(1, jt)
             store(jt)

@@ -199,25 +199,24 @@ def tile_list_rvq_silu_bias_kernel(
                 )
             nc.sync.dma_start(out=out.rearrange("(nt p) j -> p nt j", p=P)[:, :, cols], in_=res[:])
 
-        nc.gpsimd.memset(tabs[:].bitcast(I32), 0)
+        nc.vector.memset(tabs[:].bitcast(I32), 0)
         nc.vector.memset(w0s[:].rearrange("p a c -> p (a c)").bitcast(I32), 0)
         nc.vector.memset(w1s[:].rearrange("p a c -> p (a c)").bitcast(I32), 0)
         nc.vector.memset(wds[:].rearrange("p a c -> p (a c)").bitcast(I32), 0)
         nc.vector.memset(moved[:].bitcast(I32), 0)
         nc.vector.memset(ident[:], 0.0)
         nc.vector.memset(warm[:, 0, :], 0.0)
-        nc.scalar.dma_start(out=smt[:], in_=sm.rearrange("(h p i) -> p h i", h=2, i=4))
         nc.scalar.activation(out=warm[:, 1, 0:1], in_=warm[:, 0, 0:1], func=ACT.Silu)
         make_identity(nc, ident[:], nomemset=True)
 
         nc.sync.dma_start(offsets[:], offs)
+        nc.sync.dma_start(out=w0w[0][:].bitcast(I32), in_=w0_words[0].bitcast(I32))
         for r in range(4):
             nc.sync.dma_start(
                 out=tabs[r:P:16, :].bitcast(I32),
                 in_=tab_scales[:, r:16:4, :].bitcast(I32).rearrange("a q c -> q a c"),
             )
         nc.sync.dma_start(out=tabw[:], in_=tab_words[0].rearrange("p t f -> p (t f)").bitcast(I32))
-        nc.sync.dma_start(out=w0w[0][:].bitcast(I32), in_=w0_words[0].bitcast(I32))
         load_planes(w0s, w0_scales, nc.sync)
         nc.sync.dma_start(out=w0w[1][:].bitcast(I32), in_=w0_words[1].bitcast(I32))
         load_w2(0, 0, 0, HALF)
@@ -241,6 +240,7 @@ def tile_list_rvq_silu_bias_kernel(
         load_w1(1, 1, 2)
         load_w2(1, 1, 0, JH)
         load_w2(1, 1, JH, HALF)
+        nc.sync.dma_start(out=smt[:], in_=sm.rearrange("(h p i) -> p h i", h=2, i=4))
         nc.sync.dma_start(out=wdw[:].bitcast(I32), in_=wd_words.bitcast(I32).rearrange("a p c -> p a c"))
         load_planes(wds, wd_scales, nc.sync)
         with nc.allow_non_contiguous_dma(reason="one bias value to a partition"):

@@ -16,6 +16,7 @@ FP8X4 = mybir.dt.float8_e4m3fn_x4
 FP4X4 = mybir.dt.float4_e2m1fn_x4
 ACT = mybir.ActivationFunctionType
 MULT = mybir.AluOpType.mult
+ADD = mybir.AluOpType.add
 
 P = 128
 HALF = 512
@@ -43,7 +44,7 @@ def tile_list_rvq_silu_bias_kernel(
         w0s = keep.tile([P, 2, R], U8, name="w0s", align_bytes=64)
         w1w = {}
         w1s = keep.tile([P, 2, R], U8, name="w1s", align_bytes=64)
-        smt = keep.tile([P, 2, 4], F32, name="smt")
+        smt = keep.tile([P, 2, 8], F32, name="smt")
         bias = keep.tile([P, 2], F32, name="bias")
         ident = keep.tile([P, P], F32, name="ident", align_bytes=64)
         vw = {g: keep.tile([P, 2, 2 * J], U8, name=f"vw{g}", align_bytes=64) for g in range(2)}
@@ -161,7 +162,7 @@ def tile_list_rvq_silu_bias_kernel(
             nc.vector.tensor_tensor(
                 out=hgrp[hb, jt // 2][:, P * (jt % 2) : P * (jt % 2 + 1), :],
                 in0=turned[hb, jt][:].rearrange("p i j -> p j i"),
-                in1=smt[:, hb, :].unsqueeze(1).to_broadcast([P, P, 4]),
+                in1=smt[:, hb, 0:4].unsqueeze(1).to_broadcast([P, P, 4]),
                 op=MULT,
             )
 
@@ -193,10 +194,15 @@ def tile_list_rvq_silu_bias_kernel(
         def store(jt):
             cols = slice(P * jt, P * (jt + 1))
             res = keep.tile([P, 2, P], F32, name=f"res{jt}")
-            for nt in range(2):
-                nc.scalar.activation(
-                    out=res[:, nt, :], in_=y[jt][:, nt, :], func=ACT.Identity, bias=bias[:, nt : nt + 1]
+            if jt == 3:
+                nc.vector.tensor_tensor(
+                    out=res[:], in0=y[jt][:], in1=bias[:].unsqueeze(2).to_broadcast([P, 2, P]), op=ADD
                 )
+            else:
+                for nt in range(2):
+                    nc.scalar.activation(
+                        out=res[:, nt, :], in_=y[jt][:, nt, :], func=ACT.Identity, bias=bias[:, nt : nt + 1]
+                    )
             nc.sync.dma_start(out=out.rearrange("(nt p) j -> p nt j", p=P)[:, :, cols], in_=res[:])
 
         nc.vector.memset(tabs[:].bitcast(I32), 0)
@@ -229,30 +235,33 @@ def tile_list_rvq_silu_bias_kernel(
         gather_words(0, P, JH, 0)
         part_words(0, 0, P)
         part_words(0, P, JH)
-        gather_words(0, JH, J, 768)
-        gather_scales(1, 0, J)
-        load_w1(1, 0, 1)
+        gather_words(0, JH, J, 512)
+        gather_scales(1, 0, JH)
         part_words(0, JH, J)
-        gather_words(1, 0, J, 1536)
-        gather_scales(2, 0, J)
-        move_scales(1, 3)
+        gather_scales(1, JH, J)
+        move_scales(1, 2)
+        load_w1(1, 0, 1)
+        gather_words(1, 0, J, 1280)
+        gather_scales(2, 0, JH)
+        part_words(1, 0, J)
+        gather_scales(2, JH, J)
         load_w2(1, 0, 0, HALF)
+        move_scales(2, 3)
         load_w1(1, 1, 2)
         load_w2(1, 1, 0, JH)
         load_w2(1, 1, JH, HALF)
-        nc.sync.dma_start(out=smt[:], in_=sm.rearrange("(h p i) -> p h i", h=2, i=4))
+        nc.sync.dma_start(out=smt[:, :, 0:4], in_=sm.rearrange("(h p i) -> p h i", h=2, i=4))
         nc.sync.dma_start(out=wdw[:].bitcast(I32), in_=wd_words.bitcast(I32).rearrange("a p c -> p a c"))
         load_planes(wds, wd_scales, nc.sync)
         with nc.allow_non_contiguous_dma(reason="one bias value to a partition"):
             nc.sync.dma_start(out=bias[:], in_=b.rearrange("(nt p) -> p nt", p=P))
-        part_words(1, 0, J)
-        gather_words(2, 0, J, 1536)
+        gather_words(2, 0, J, 1280)
 
         cast_w2(0, 0, 0, HALF, HALF)
         quantize_w2(0, 0, 0, HALF)
-        vw[2] = keep.tile([P, 2, 2 * J], U8, name="vw2", tag="grp000", align_bytes=64)
+        vw[2] = keep.tile([P, 2, 2 * J], U8, name="vw2", tag="raw000", align_bytes=64)
         part_words(2, 0, J)
-        cast_w2(0, 1, 0, HALF, 320)
+        cast_w2(0, 1, 0, HALF, 512)
         quantize_w2(0, 1, 0, HALF)
         cast_w2(1, 0, 0, HALF, 0)
         quantize_w2(1, 0, 0, HALF)

@@ -175,35 +175,43 @@ def tile_list_rvq_silu_bias_kernel(
             )
 
         y = {}
+        ysum = {}
 
         def second_layer(hb, jt):
             cols = slice(P * jt, P * (jt + 1))
             if hb == 0:
-                y[jt] = psum.tile([P, 2, P], F32, name=f"y{jt}", tag=f"bank1{jt}")
+                y[jt] = psum.tile([P, 2, P], F32, name=f"y{jt}", tag=f"bank0{jt}")
+                ysum[jt, 0], ysum[jt, 1] = y[jt][:, 0, :], y[jt][:, 1, :]
+                if jt == 3:
+                    y[4] = psum.tile([P, P], F32, name="y4", tag="bank10")
+                    ysum[jt, 1] = y[4][:]
             for nt in range(2):
                 nc.tensor.matmul_mx(
-                    out=y[jt][:, nt, :],
+                    out=ysum[jt, nt],
                     lhsT=wdw[:, hb, 2 * P * nt : 2 * P * (nt + 1)].bitcast(FP4X4),
                     lhsT_scale=wds[:, hb, P * nt : P * (nt + 1)],
                     rhs=hc[hb][:, cols].bitcast(FP8X4),
                     rhs_scale=hs[hb][:, cols],
-                    start=(hb == 0 and nt == 0),
-                    stop=(hb == 1 and nt == 1),
+                    start=(hb == 0 and (nt == 0 or jt == 3)),
+                    stop=(hb == 1 and (nt == 1 or jt == 3)),
                 )
 
         def store(jt):
             cols = slice(P * jt, P * (jt + 1))
-            res = keep.tile([P, 2, P], F32, name=f"res{jt}")
             if jt == 3:
-                nc.vector.tensor_tensor(
-                    out=res[:], in0=y[jt][:], in1=bias[:].unsqueeze(2).to_broadcast([P, 2, P]), op=ADD
-                )
+                lo = keep.tile([P, P], F32, name="res3lo")
+                hi = keep.tile([P, P], F32, name="res3hi")
+                nc.vector.tensor_scalar(out=lo[:], in0=ysum[jt, 0], scalar1=bias[:, 0:1], scalar2=None, op0=ADD)
+                nc.sync.dma_start(out=out[0:P, cols], in_=lo[:])
+                nc.scalar.activation(out=hi[:], in_=ysum[jt, 1], func=ACT.Identity, bias=bias[:, 1:2])
+                nc.scalar.dma_start(out=out[P : 2 * P, cols], in_=hi[:])
             else:
+                res = keep.tile([P, 2, P], F32, name=f"res{jt}")
                 for nt in range(2):
                     nc.scalar.activation(
-                        out=res[:, nt, :], in_=y[jt][:, nt, :], func=ACT.Identity, bias=bias[:, nt : nt + 1]
+                        out=res[:, nt, :], in_=ysum[jt, nt], func=ACT.Identity, bias=bias[:, nt : nt + 1]
                     )
-            nc.sync.dma_start(out=out.rearrange("(nt p) j -> p nt j", p=P)[:, :, cols], in_=res[:])
+                nc.sync.dma_start(out=out.rearrange("(nt p) j -> p nt j", p=P)[:, :, cols], in_=res[:])
 
         nc.vector.memset(tabs[:].bitcast(I32), 0)
         nc.vector.memset(w0s[:].rearrange("p a c -> p (a c)").bitcast(I32), 0)
@@ -282,20 +290,24 @@ def tile_list_rvq_silu_bias_kernel(
         for jt in range(4):
             first_layer(2, 1, 0, jt, last=True)
             silu(0, jt)
-        cast_w2(1, 1, JH, HALF, 128)
+        cast_w2(1, 1, JH, HALF, 192)
         quantize_w2(1, 1, JH, HALF)
-        hgrp[0, 0] = keep.tile([P, JH, 4], BF16, name="hgrp00", tag=f"grp11{JH}", align_bytes=64)
-        hgrp[0, 1] = keep.tile([P, JH, 4], BF16, name="hgrp01", tag=f"raw11{JH}", align_bytes=64)
+        hgrp[0, 0] = keep.tile([P, JH, 4], BF16, name="hgrp00", align_bytes=64)
+        hgrp[0, 1] = keep.tile([P, JH, 4], BF16, name="hgrp01", align_bytes=64)
         hgrp[1, 0] = keep.tile([P, JH, 4], BF16, name="hgrp10", align_bytes=64)
         hgrp[1, 1] = keep.tile([P, JH, 4], BF16, name="hgrp11", align_bytes=64)
         for jt in range(4):
             first_layer(1, 1, 1, jt)
         for jt in range(4):
             turn(0, jt)
-        for jt in range(4):
+        for jt in range(2):
             first_layer(2, 0, 1, jt)
-        for jt in range(4):
+        for jt in range(2):
             first_layer(2, 1, 1, jt, last=True)
+            silu(1, jt)
+        for jt in range(2, 4):
+            first_layer(2, 1, 1, jt)
+            first_layer(2, 0, 1, jt, last=True)
             silu(1, jt)
         for jt in range(4):
             smooth(0, jt)
@@ -308,5 +320,6 @@ def tile_list_rvq_silu_bias_kernel(
             quantize_h(1, jt, jt + 1)
         for jt in range(4):
             second_layer(0, jt)
+        for jt in range(4):
             second_layer(1, jt)
             store(jt)

@@ -147,6 +147,8 @@ def tile_list_rvq_silu_bias_kernel(
         act = {}
         turned = {}
 
+        hbuf = {}
+
         def silu(hb, jt):
             act[hb, jt] = keep.tile([P, 4, P], F32, name=f"act{hb}{jt}", align_bytes=64)
             nc.scalar.activation(
@@ -160,10 +162,21 @@ def tile_list_rvq_silu_bias_kernel(
 
         def smooth(hb, jt):
             nc.vector.tensor_tensor(
-                out=hgrp[hb, jt // 2][:, P * (jt % 2) : P * (jt % 2 + 1), :],
+                out=hbuf[hb, jt],
                 in0=turned[hb, jt][:].rearrange("p i j -> p j i"),
                 in1=smt[:, hb, 0:4].unsqueeze(1).to_broadcast([P, P, 4]),
                 op=MULT,
+            )
+
+        def smooth_shared(hb, jt):
+            prod = keep.tile([P, 4, P], F32, name=f"prod{hb}{jt}", align_bytes=64)
+            for i in range(4):
+                nc.scalar.activation(
+                    out=prod[:, i, :], in_=turned[hb, jt][:, i, :], func=ACT.Copy, scale=smt[:, hb, i : i + 1]
+                )
+            nc.vector.tensor_copy(
+                out=hbuf[hb, jt].rearrange("p (c e) i -> p c i e", e=4),
+                in_=prod[:].rearrange("p i (c e) -> p c i e", e=4),
             )
 
         def quantize_h(hb, jt0, jt1):
@@ -171,47 +184,39 @@ def tile_list_rvq_silu_bias_kernel(
             nc.vector.quantize_mx(
                 out=hc[hb][:, cols].bitcast(FP8X4),
                 scales=hs[hb][:, cols],
-                in_=hgrp[hb, jt0 // 2][:, P * (jt0 % 2) : P * (jt0 % 2 + jt1 - jt0), :].rearrange("p j i -> p (j i)"),
+                in_=(hbuf[hb, jt0] if hb else hgrp[hb, jt0 // 2][:]).rearrange("p j i -> p (j i)"),
             )
 
         y = {}
-        ysum = {}
 
         def second_layer(hb, jt):
             cols = slice(P * jt, P * (jt + 1))
             if hb == 0:
                 y[jt] = psum.tile([P, 2, P], F32, name=f"y{jt}", tag=f"bank0{jt}")
-                ysum[jt, 0], ysum[jt, 1] = y[jt][:, 0, :], y[jt][:, 1, :]
-                if jt == 3:
-                    y[4] = psum.tile([P, P], F32, name="y4", tag="bank10")
-                    ysum[jt, 1] = y[4][:]
             for nt in range(2):
                 nc.tensor.matmul_mx(
-                    out=ysum[jt, nt],
+                    out=y[jt][:, nt, :],
                     lhsT=wdw[:, hb, 2 * P * nt : 2 * P * (nt + 1)].bitcast(FP4X4),
                     lhsT_scale=wds[:, hb, P * nt : P * (nt + 1)],
                     rhs=hc[hb][:, cols].bitcast(FP8X4),
                     rhs_scale=hs[hb][:, cols],
-                    start=(hb == 0 and (nt == 0 or jt == 3)),
-                    stop=(hb == 1 and (nt == 1 or jt == 3)),
+                    start=(hb == 0 and nt == 0),
+                    stop=(hb == 1 and nt == 1),
                 )
 
         def store(jt):
             cols = slice(P * jt, P * (jt + 1))
+            res = keep.tile([P, 2, P], F32, name=f"res{jt}")
             if jt == 3:
-                lo = keep.tile([P, P], F32, name="res3lo")
-                hi = keep.tile([P, P], F32, name="res3hi")
-                nc.vector.tensor_scalar(out=lo[:], in0=ysum[jt, 0], scalar1=bias[:, 0:1], scalar2=None, op0=ADD)
-                nc.sync.dma_start(out=out[0:P, cols], in_=lo[:])
-                nc.scalar.activation(out=hi[:], in_=ysum[jt, 1], func=ACT.Identity, bias=bias[:, 1:2])
-                nc.scalar.dma_start(out=out[P : 2 * P, cols], in_=hi[:])
+                nc.vector.tensor_tensor(
+                    out=res[:], in0=y[jt][:], in1=bias[:].unsqueeze(2).to_broadcast([P, 2, P]), op=ADD
+                )
             else:
-                res = keep.tile([P, 2, P], F32, name=f"res{jt}")
                 for nt in range(2):
                     nc.scalar.activation(
-                        out=res[:, nt, :], in_=ysum[jt, nt], func=ACT.Identity, bias=bias[:, nt : nt + 1]
+                        out=res[:, nt, :], in_=y[jt][:, nt, :], func=ACT.Identity, bias=bias[:, nt : nt + 1]
                     )
-                nc.sync.dma_start(out=out.rearrange("(nt p) j -> p nt j", p=P)[:, :, cols], in_=res[:])
+            nc.sync.dma_start(out=out.rearrange("(nt p) j -> p nt j", p=P)[:, :, cols], in_=res[:])
 
         nc.vector.memset(tabs[:].bitcast(I32), 0)
         nc.vector.memset(w0s[:].rearrange("p a c -> p (a c)").bitcast(I32), 0)
@@ -290,12 +295,12 @@ def tile_list_rvq_silu_bias_kernel(
         for jt in range(4):
             first_layer(2, 1, 0, jt, last=True)
             silu(0, jt)
-        cast_w2(1, 1, JH, HALF, 192)
+        cast_w2(1, 1, JH, HALF, 128)
         quantize_w2(1, 1, JH, HALF)
-        hgrp[0, 0] = keep.tile([P, JH, 4], BF16, name="hgrp00", align_bytes=64)
-        hgrp[0, 1] = keep.tile([P, JH, 4], BF16, name="hgrp01", align_bytes=64)
-        hgrp[1, 0] = keep.tile([P, JH, 4], BF16, name="hgrp10", align_bytes=64)
-        hgrp[1, 1] = keep.tile([P, JH, 4], BF16, name="hgrp11", align_bytes=64)
+        hgrp[0, 0] = keep.tile([P, JH, 4], BF16, name="hgrp00", tag=f"grp11{JH}", align_bytes=64)
+        hgrp[0, 1] = keep.tile([P, JH, 4], BF16, name="hgrp01", tag=f"raw11{JH}", align_bytes=64)
+        for jt in range(4):
+            hbuf[0, jt] = hgrp[0, jt // 2][:, P * (jt % 2) : P * (jt % 2 + 1), :]
         for jt in range(4):
             first_layer(1, 1, 1, jt)
         for jt in range(4):
@@ -309,17 +314,19 @@ def tile_list_rvq_silu_bias_kernel(
             first_layer(2, 1, 1, jt)
             first_layer(2, 0, 1, jt, last=True)
             silu(1, jt)
-        for jt in range(4):
+        for jt in range(3):
             smooth(0, jt)
-            if jt % 2 == 1:
-                quantize_h(0, jt - 1, jt + 1)
+        quantize_h(0, 0, 2)
+        smooth_shared(0, 3)
+        quantize_h(0, 2, 4)
         for jt in range(4):
             turn(1, jt)
         for jt in range(4):
+            second_layer(0, jt)
+        for jt in range(4):
+            hbuf[1, jt] = keep.tile([P, P, 4], BF16, name=f"hbuf1{jt}", align_bytes=64)[:]
             smooth(1, jt)
             quantize_h(1, jt, jt + 1)
-        for jt in range(4):
-            second_layer(0, jt)
         for jt in range(4):
             second_layer(1, jt)
             store(jt)

@@ -115,6 +115,19 @@ def tile_list_rvq_silu_bias_kernel(
             if cut < (c1 - c0) // 4:
                 nc.vector.tensor_copy(out=dst[:, cut:], in_=src[:, cut:])
 
+        def cast_and_quantize_in_halves(hb, a, c1):
+            grp[hb, a, 0] = keep.tile([P, c1, 4], BF16, name=f"grp{hb}{a}0", tag=f"grp{hb}{a}0", align_bytes=64)
+            dst = grp[hb, a, 0][:].rearrange("p (c e) i -> p c i e", e=4)
+            src = raw[hb, a, 0][:].rearrange("p i (c e) -> p c i e", e=4)
+            for lo in (0, c1 // 8):
+                nc.vector.tensor_copy(out=dst[:, lo : lo + c1 // 8], in_=src[:, lo : lo + c1 // 8])
+            for lo in (0, c1 // 2):
+                nc.vector.quantize_mx(
+                    out=w2c[hb, a][:, lo : lo + c1 // 2].bitcast(FP8X4),
+                    scales=w2s[hb, a][:, lo : lo + c1 // 2],
+                    in_=grp[hb, a, 0][:, lo : lo + c1 // 2, :].rearrange("p c i -> p (c i)"),
+                )
+
         def quantize_w2(hb, a, c0, c1):
             nc.vector.quantize_mx(
                 out=w2c[hb, a][:, c0:c1].bitcast(FP8X4),
@@ -276,10 +289,8 @@ def tile_list_rvq_silu_bias_kernel(
         part_words(2, 0, J)
         cast_w2(0, 1, 0, HALF, 512)
         quantize_w2(0, 1, 0, HALF)
-        cast_w2(1, 0, 0, HALF, 0)
-        quantize_w2(1, 0, 0, HALF)
-        cast_w2(1, 1, 0, JH, 0)
-        quantize_w2(1, 1, 0, JH)
+        cast_and_quantize_in_halves(1, 0, HALF)
+        cast_and_quantize_in_halves(1, 1, JH)
 
         for a in range(2):
             for jt in range(4):
@@ -295,7 +306,7 @@ def tile_list_rvq_silu_bias_kernel(
         for jt in range(4):
             first_layer(2, 1, 0, jt, last=True)
             silu(0, jt)
-        cast_w2(1, 1, JH, HALF, 128)
+        cast_w2(1, 1, JH, HALF, 96)
         quantize_w2(1, 1, JH, HALF)
         hgrp[0, 0] = keep.tile([P, JH, 4], BF16, name="hgrp00", tag=f"grp11{JH}", align_bytes=64)
         hgrp[0, 1] = keep.tile([P, JH, 4], BF16, name="hgrp01", tag=f"raw11{JH}", align_bytes=64)
@@ -316,8 +327,8 @@ def tile_list_rvq_silu_bias_kernel(
             silu(1, jt)
         for jt in range(3):
             smooth(0, jt)
-        quantize_h(0, 0, 2)
         smooth_shared(0, 3)
+        quantize_h(0, 0, 2)
         quantize_h(0, 2, 4)
         for jt in range(4):
             turn(1, jt)

from contextlib import ExitStack

import concourse.mybir as mybir
from concourse.masks import make_identity

K, R, N, T, J = 1024, 1024, 256, 1024, 512
FLOPS = 2 * J * (3 * K * R + R * N)

F32 = mybir.dt.float32
BF16 = mybir.dt.bfloat16
I32 = mybir.dt.int32
U32 = mybir.dt.uint32
U16 = mybir.dt.uint16
U8 = mybir.dt.uint8
FP8X4 = mybir.dt.float8_e4m3fn_x4
FP4X4 = mybir.dt.float4_e2m1fn_x4
ACT = mybir.ActivationFunctionType
MULT = mybir.AluOpType.mult
ADD = mybir.AluOpType.add

P = 128
HALF = 512
JH = J // 2
SCALES_AT = (4096, 0, 512)


def tile_list_rvq_silu_bias_kernel(
    tc, tab_words, tab_scales, w0_words, w0_scales, w1_words, w1_scales, w2, sm, wd_words, wd_scales, b, offs, out
):
    nc = tc.nc
    with ExitStack() as ctx:
        keep = ctx.enter_context(tc.tile_pool(name="keep", bufs=1))
        psum = ctx.enter_context(tc.psum_pool(name="psum", bufs=1))

        offsets = keep.tile([P, 3 * J // 16], U16, name="offsets")
        tabw = keep.tile([P, T], I32, name="tabw", align_bytes=64)
        tabs = keep.tile([P, T], U8, name="tabs", align_bytes=64)
        picked = keep.tile([P, 4608], U8, name="picked", align_bytes=64)
        moved = keep.tile([P, 3 * J], U8, name="moved", align_bytes=64)
        warm = keep.tile([P, 2, 8], F32, name="warm")
        wdw = keep.tile([P, 2, 2 * N], U8, name="wdw", align_bytes=64)
        wds = keep.tile([P, 2, N], U8, name="wds", align_bytes=64)
        w0w = [keep.tile([P, 2 * R], U8, name=f"w0w{a}", align_bytes=64) for a in range(2)]
        w0s = keep.tile([P, 2, R], U8, name="w0s", align_bytes=64)
        w1w = {}
        w1s = keep.tile([P, 2, R], U8, name="w1s", align_bytes=64)
        smt = keep.tile([P, 2, 8], F32, name="smt")
        bias = keep.tile([P, 2], F32, name="bias")
        ident = keep.tile([P, P], F32, name="ident", align_bytes=64)
        vw = {g: keep.tile([P, 2, 2 * J], U8, name=f"vw{g}", align_bytes=64) for g in range(2)}
        raw = {}
        staged = {}
        grp = {}
        w2c = {}
        w2s = {}
        for hb in range(2):
            for a in range(2):
                w2c[hb, a] = keep.tile([P, HALF], U32, name=f"w2c{hb}{a}", align_bytes=64)
                w2s[hb, a] = keep.tile([P, HALF], U8, name=f"w2s{hb}{a}", align_bytes=64)
        hgrp = {}
        hc = [keep.tile([P, J], U32, name=f"hc{hb}", align_bytes=64) for hb in range(2)]
        hs = [keep.tile([P, J], U8, name=f"hs{hb}", align_bytes=64) for hb in range(2)]
        acc = {}
        for hb in range(2):
            for jt in range(4):
                acc[hb, jt] = psum.tile([P, HALF], F32, name=f"acc{hb}{jt}", tag=f"bank{hb}{jt}")

        def load_planes(plane, scales, queue):
            for r in range(4):
                queue.dma_start(
                    out=plane[r:P:32, :, :].bitcast(I32),
                    in_=scales[:, r:16:4, :].bitcast(I32).rearrange("a q c -> q a c"),
                )

        def load_w2(hb, a, c0, c1):
            raw[hb, a, c0] = keep.tile([P, 4, c1 - c0], F32, name=f"raw{hb}{a}{c0}", tag=f"raw{hb}{a}{c0}", align_bytes=64)
            rows = w2[HALF * a : HALF * (a + 1), HALF * hb + c0 : HALF * hb + c1]
            nc.sync.dma_start(out=raw[hb, a, c0][:], in_=rows.rearrange("(p i) c -> p i c", i=4))

        def load_w1(a, hb0, hb1):
            words = keep.tile([P, 4 * HALF * (hb1 - hb0)], U8, name=f"w1w{a}{hb0}", align_bytes=64)
            for hb in range(hb0, hb1):
                w1w[hb, a] = words[:, 4 * HALF * (hb - hb0) : 4 * HALF * (hb - hb0 + 1)]
            cols = w1_words[a, :, HALF * hb0 : HALF * hb1, :]
            nc.sync.dma_start(out=words[:].bitcast(I32), in_=cols.rearrange("p r i -> p (r i)").bitcast(I32))

        def places(g, j0, j1):
            return offsets[:, (g * J + j0) // 16 : (g * J + j1) // 16]

        def gather_scales(g, j0, j1):
            dst = picked[:, SCALES_AT[g] + j0 : SCALES_AT[g] + j1]
            nc.vector.tensor_copy(out=dst, in_=tabs[:].indirect(places(g, j0, j1)))

        def move_scales(g0, g1):
            src = picked[16:128, SCALES_AT[g0] : SCALES_AT[g0] + J * (g1 - g0)]
            nc.sync.dma_start(out=moved[0:112, J * g0 : J * g1].bitcast(I32), in_=src.bitcast(I32))

        def gather_words(g, j0, j1, at):
            staged[g, j0] = picked[:, at : at + 4 * (j1 - j0)]
            nc.vector.tensor_copy(out=staged[g, j0].bitcast(U32), in_=tabw[:].bitcast(U32).indirect(places(g, j0, j1)))

        def part_words(g, j0, j1):
            nc.vector.tensor_copy(
                out=vw[g][:, :, 2 * j0 : 2 * j1].bitcast(U16),
                in_=staged[g, j0].bitcast(U16).rearrange("p (j d) -> p d j", d=2),
            )

        def cast_w2(hb, a, c0, c1, on_scalar):
            grp[hb, a, c0] = keep.tile([P, c1 - c0, 4], BF16, name=f"grp{hb}{a}{c0}", tag=f"grp{hb}{a}{c0}", align_bytes=64)
            dst = grp[hb, a, c0][:].rearrange("p (c e) i -> p c i e", e=4)
            src = raw[hb, a, c0][:].rearrange("p i (c e) -> p c i e", e=4)
            cut = on_scalar // 4
            if cut > 0:
                nc.scalar.copy(out=dst[:, :cut], in_=src[:, :cut])
            if cut < (c1 - c0) // 4:
                nc.vector.tensor_copy(out=dst[:, cut:], in_=src[:, cut:])

        def cast_and_quantize_in_halves(hb, a, c1):
            grp[hb, a, 0] = keep.tile([P, c1, 4], BF16, name=f"grp{hb}{a}0", tag=f"grp{hb}{a}0", align_bytes=64)
            dst = grp[hb, a, 0][:].rearrange("p (c e) i -> p c i e", e=4)
            src = raw[hb, a, 0][:].rearrange("p i (c e) -> p c i e", e=4)
            for lo in (0, c1 // 8):
                nc.vector.tensor_copy(out=dst[:, lo : lo + c1 // 8], in_=src[:, lo : lo + c1 // 8])
            for lo in (0, c1 // 2):
                nc.vector.quantize_mx(
                    out=w2c[hb, a][:, lo : lo + c1 // 2].bitcast(FP8X4),
                    scales=w2s[hb, a][:, lo : lo + c1 // 2],
                    in_=grp[hb, a, 0][:, lo : lo + c1 // 2, :].rearrange("p c i -> p (c i)"),
                )

        def quantize_w2(hb, a, c0, c1):
            nc.vector.quantize_mx(
                out=w2c[hb, a][:, c0:c1].bitcast(FP8X4),
                scales=w2s[hb, a][:, c0:c1],
                in_=grp[hb, a, c0][:].rearrange("p c i -> p (c i)"),
            )

        def first_layer(g, a, hb, jt, last=False):
            cols = slice(HALF * hb, HALF * (hb + 1))
            if g == 0:
                rhs, rhs_scale = w0w[a][:, 2 * cols.start : 2 * cols.stop].bitcast(FP4X4), w0s[:, a, cols]
            elif g == 1:
                rhs, rhs_scale = w1w[hb, a].bitcast(FP8X4), w1s[:, a, cols]
            else:
                rhs, rhs_scale = w2c[hb, a][:].bitcast(FP8X4), w2s[hb, a][:]
            if a == 0:
                lhsT_scale = picked[:, SCALES_AT[g] + P * jt : SCALES_AT[g] + P * (jt + 1)]
            else:
                lhsT_scale = moved[:, J * g + P * jt : J * g + P * (jt + 1)]
            nc.tensor.matmul_mx(
                out=acc[hb, jt][:],
                lhsT=vw[g][:, a, 2 * P * jt : 2 * P * (jt + 1)].bitcast(FP4X4),
                lhsT_scale=lhsT_scale,
                rhs=rhs,
                rhs_scale=rhs_scale,
                start=(g == 0 and a == 0),
                stop=last,
            )

        act = {}
        turned = {}

        hbuf = {}

        def silu(hb, jt):
            act[hb, jt] = keep.tile([P, 4, P], F32, name=f"act{hb}{jt}", align_bytes=64)
            nc.scalar.activation(
                out=act[hb, jt][:], in_=acc[hb, jt][:].rearrange("p (q i) -> p i q", i=4), func=ACT.Silu
            )

        def turn(hb, jt):
            turned[hb, jt] = psum.tile([P, 4, P], F32, name=f"turned{hb}{jt}", tag=f"bank{hb}{jt}")
            for i in range(4):
                nc.tensor.transpose(turned[hb, jt][:, i, :], act[hb, jt][:, i, :], ident[:])

        def smooth(hb, jt):
            nc.vector.tensor_tensor(
                out=hbuf[hb, jt],
                in0=turned[hb, jt][:].rearrange("p i j -> p j i"),
                in1=smt[:, hb, 0:4].unsqueeze(1).to_broadcast([P, P, 4]),
                op=MULT,
            )

        def smooth_shared(hb, jt):
            prod = keep.tile([P, 4, P], F32, name=f"prod{hb}{jt}", align_bytes=64)
            for i in range(4):
                nc.scalar.activation(
                    out=prod[:, i, :], in_=turned[hb, jt][:, i, :], func=ACT.Copy, scale=smt[:, hb, i : i + 1]
                )
            nc.vector.tensor_copy(
                out=hbuf[hb, jt].rearrange("p (c e) i -> p c i e", e=4),
                in_=prod[:].rearrange("p i (c e) -> p c i e", e=4),
            )

        def quantize_h(hb, jt0, jt1):
            cols = slice(P * jt0, P * jt1)
            nc.vector.quantize_mx(
                out=hc[hb][:, cols].bitcast(FP8X4),
                scales=hs[hb][:, cols],
                in_=(hbuf[hb, jt0] if hb else hgrp[hb, jt0 // 2][:]).rearrange("p j i -> p (j i)"),
            )

        y = {}

        def second_layer(hb, jt):
            cols = slice(P * jt, P * (jt + 1))
            if hb == 0:
                y[jt] = psum.tile([P, 2, P], F32, name=f"y{jt}", tag=f"bank0{jt}")
            for nt in range(2):
                nc.tensor.matmul_mx(
                    out=y[jt][:, nt, :],
                    lhsT=wdw[:, hb, 2 * P * nt : 2 * P * (nt + 1)].bitcast(FP4X4),
                    lhsT_scale=wds[:, hb, P * nt : P * (nt + 1)],
                    rhs=hc[hb][:, cols].bitcast(FP8X4),
                    rhs_scale=hs[hb][:, cols],
                    start=(hb == 0 and nt == 0),
                    stop=(hb == 1 and nt == 1),
                )

        def store(jt):
            cols = slice(P * jt, P * (jt + 1))
            res = keep.tile([P, 2, P], F32, name=f"res{jt}")
            if jt == 3:
                nc.vector.tensor_tensor(
                    out=res[:], in0=y[jt][:], in1=bias[:].unsqueeze(2).to_broadcast([P, 2, P]), op=ADD
                )
            else:
                for nt in range(2):
                    nc.scalar.activation(
                        out=res[:, nt, :], in_=y[jt][:, nt, :], func=ACT.Identity, bias=bias[:, nt : nt + 1]
                    )
            nc.sync.dma_start(out=out.rearrange("(nt p) j -> p nt j", p=P)[:, :, cols], in_=res[:])

        nc.vector.memset(tabs[:].bitcast(I32), 0)
        nc.vector.memset(w0s[:].rearrange("p a c -> p (a c)").bitcast(I32), 0)
        nc.vector.memset(w1s[:].rearrange("p a c -> p (a c)").bitcast(I32), 0)
        nc.vector.memset(wds[:].rearrange("p a c -> p (a c)").bitcast(I32), 0)
        nc.vector.memset(moved[:].bitcast(I32), 0)
        nc.vector.memset(ident[:], 0.0)
        nc.vector.memset(warm[:, 0, :], 0.0)
        nc.scalar.activation(out=warm[:, 1, 0:1], in_=warm[:, 0, 0:1], func=ACT.Silu)
        make_identity(nc, ident[:], nomemset=True)

        nc.sync.dma_start(offsets[:], offs)
        nc.sync.dma_start(out=w0w[0][:].bitcast(I32), in_=w0_words[0].bitcast(I32))
        for r in range(4):
            nc.sync.dma_start(
                out=tabs[r:P:16, :].bitcast(I32),
                in_=tab_scales[:, r:16:4, :].bitcast(I32).rearrange("a q c -> q a c"),
            )
        nc.sync.dma_start(out=tabw[:], in_=tab_words[0].rearrange("p t f -> p (t f)").bitcast(I32))
        load_planes(w0s, w0_scales, nc.sync)
        nc.sync.dma_start(out=w0w[1][:].bitcast(I32), in_=w0_words[1].bitcast(I32))
        load_w2(0, 0, 0, HALF)
        gather_scales(0, 0, J)
        move_scales(0, 1)
        load_planes(w1s, w1_scales, nc.sync)
        load_w1(0, 0, 2)
        load_w2(0, 1, 0, HALF)
        gather_words(0, 0, P, 1280)
        gather_words(0, P, JH, 0)
        part_words(0, 0, P)
        part_words(0, P, JH)
        gather_words(0, JH, J, 512)
        gather_scales(1, 0, JH)
        part_words(0, JH, J)
        gather_scales(1, JH, J)
        move_scales(1, 2)
        load_w1(1, 0, 1)
        gather_words(1, 0, J, 1280)
        gather_scales(2, 0, JH)
        part_words(1, 0, J)
        gather_scales(2, JH, J)
        load_w2(1, 0, 0, HALF)
        move_scales(2, 3)
        load_w1(1, 1, 2)
        load_w2(1, 1, 0, JH)
        load_w2(1, 1, JH, HALF)
        nc.sync.dma_start(out=smt[:, :, 0:4], in_=sm.rearrange("(h p i) -> p h i", h=2, i=4))
        nc.sync.dma_start(out=wdw[:].bitcast(I32), in_=wd_words.bitcast(I32).rearrange("a p c -> p a c"))
        load_planes(wds, wd_scales, nc.sync)
        with nc.allow_non_contiguous_dma(reason="one bias value to a partition"):
            nc.sync.dma_start(out=bias[:], in_=b.rearrange("(nt p) -> p nt", p=P))
        gather_words(2, 0, J, 1280)

        cast_w2(0, 0, 0, HALF, HALF)
        quantize_w2(0, 0, 0, HALF)
        vw[2] = keep.tile([P, 2, 2 * J], U8, name="vw2", tag="raw000", align_bytes=64)
        part_words(2, 0, J)
        cast_w2(0, 1, 0, HALF, 512)
        quantize_w2(0, 1, 0, HALF)
        cast_and_quantize_in_halves(1, 0, HALF)
        cast_and_quantize_in_halves(1, 1, JH)

        for a in range(2):
            for jt in range(4):
                for hb in range(2):
                    first_layer(0, a, hb, jt)
        for hb in range(2):
            for jt in range(4):
                first_layer(1, 0, hb, jt)
        for jt in range(4):
            first_layer(1, 1, 0, jt)
        for jt in range(4):
            first_layer(2, 0, 0, jt)
        for jt in range(4):
            first_layer(2, 1, 0, jt, last=True)
            silu(0, jt)
        cast_w2(1, 1, JH, HALF, 96)
        quantize_w2(1, 1, JH, HALF)
        hgrp[0, 0] = keep.tile([P, JH, 4], BF16, name="hgrp00", tag=f"grp11{JH}", align_bytes=64)
        hgrp[0, 1] = keep.tile([P, JH, 4], BF16, name="hgrp01", tag=f"raw11{JH}", align_bytes=64)
        for jt in range(4):
            hbuf[0, jt] = hgrp[0, jt // 2][:, P * (jt % 2) : P * (jt % 2 + 1), :]
        for jt in range(4):
            first_layer(1, 1, 1, jt)
        for jt in range(4):
            turn(0, jt)
        for jt in range(2):
            first_layer(2, 0, 1, jt)
        for jt in range(2):
            first_layer(2, 1, 1, jt, last=True)
            silu(1, jt)
        for jt in range(2, 4):
            first_layer(2, 1, 1, jt)
            first_layer(2, 0, 1, jt, last=True)
            silu(1, jt)
        for jt in range(3):
            smooth(0, jt)
        smooth_shared(0, 3)
        quantize_h(0, 0, 2)
        quantize_h(0, 2, 4)
        for jt in range(4):
            turn(1, jt)
        for jt in range(4):
            second_layer(0, jt)
        for jt in range(4):
            hbuf[1, jt] = keep.tile([P, P, 4], BF16, name=f"hbuf1{jt}", align_bytes=64)[:]
            smooth(1, jt)
            quantize_h(1, jt, jt + 1)
        for jt in range(4):
            second_layer(1, jt)
            store(jt)
